import numpy as np
import ml_dtypes


def mxq(x, axis, fmt="e4m3"):
    dtype, down = {"e4m3": (ml_dtypes.float8_e4m3fn, 7), "e5m2": (ml_dtypes.float8_e5m2, 14)}[fmt]
    v = np.moveaxis(np.asarray(x, np.float32).astype(ml_dtypes.bfloat16).astype(np.float64), axis, -1)
    blocks = v.reshape(v.shape[:-1] + (-1, 32))
    amax = np.abs(blocks).max(-1, keepdims=True)
    byte = np.maximum(np.where(amax > 0, np.frexp(amax)[1] - 1 + 127, 0) - down, 1)
    scale = np.exp2(byte - 127.0)
    codes = (blocks / scale).astype(np.float32).astype(dtype).astype(np.float64)
    return np.moveaxis((codes * scale).reshape(v.shape), -1, axis)


WIDE = False


def mx_kscale(k):
    if not WIDE:
        return np.ones(k)
    levels = np.array([24, -24, 12, -12, 0])
    if k % 512:
        return np.exp2(np.random.permutation(np.resize(levels, k // 32))).repeat(32)
    a = np.empty((k // 512, 16))
    for p in range(k // 512):
        a[p, :8] = np.random.permutation(np.resize(levels, 8))
        for g in range(8):
            far = levels[np.abs(levels - a[p, g]) >= 10]
            a[p, g + 8] = far[np.random.randint(len(far))]
    return np.exp2(a.ravel()).repeat(32)


def f64(x):
    return np.asarray(x).astype(np.float64)


def striped(idx):
    return np.tile(idx.reshape(-1, 16).T, (8, 1)).astype(np.uint16)


def unstriped(offs):
    return offs[:16].T.reshape(-1).astype(np.int64)


E2M1 = np.array([0.0, 0.5, 1.0, 1.5, 2.0, 3.0, 4.0, 6.0, -0.0, -0.5, -1.0, -1.5, -2.0, -3.0, -4.0, -6.0])


def pack_weight(w, fmt):
    k, n = w.shape
    w = f64(np.asarray(w, np.float32).astype(ml_dtypes.bfloat16)).reshape(k // 32, 32, n)
    amax = np.abs(w).max(1)
    if fmt == "e4m3":
        byte = np.frexp(amax)[1] - 1 + 127 - 7
    else:
        mant, ex = np.frexp(amax / 6.0)
        byte = np.where(mant > 0.5, ex, ex - 1) + 127
    byte = np.clip(np.where(amax > 0, byte, 1), 1, 254)
    scaled = (w * np.exp2(127.0 - byte)[:, None, :]).reshape(k, n).astype(np.float32)
    by_word = np.ascontiguousarray(scaled.reshape(k // 512, 128, 4, n).transpose(0, 1, 3, 2))
    if fmt == "e4m3":
        words = by_word.astype(ml_dtypes.float8_e4m3fn).view(np.uint8)
    else:
        c = by_word.astype(ml_dtypes.float4_e2m1fn).view(np.uint8) & 0xF
        words = (c[..., 0::2] | (c[..., 1::2] << 4)).reshape(k // 512, 128, 2 * n)
    return np.ascontiguousarray(words), np.ascontiguousarray(byte.astype(np.uint8).reshape(k // 512, 16, n))


def unpack_weight(words, scales, fmt):
    g, _, n = scales.shape
    words = np.ascontiguousarray(words).reshape(g, 128, n, -1)
    if fmt == "e4m3":
        vals = words.view(ml_dtypes.float8_e4m3fn).astype(np.float64)
    else:
        nib = np.empty((g, 128, n, 4), np.uint8)
        nib[..., 0::2] = words & 0xF
        nib[..., 1::2] = words >> 4
        vals = E2M1[nib]
    vals = vals * np.repeat(np.exp2(scales.astype(np.float64) - 127.0), 8, axis=1)[..., None]
    return vals.transpose(0, 1, 3, 2).reshape(g * 512, n)


def gelu(f):
    return 0.5 * f * (1.0 + np.tanh(np.sqrt(2.0 / np.pi) * (f + 0.044715 * f**3)))


K, R, N, T, J = 512, 512, 512, 2048, 1024


def setup_inputs():
    n = np.random.standard_normal
    s = mx_kscale(K)[:, None]
    u = mx_kscale(R)[:, None]
    p_tab = pack_weight(n((K, T)) * s, "e4m3")
    p_wu = pack_weight(n((K, R)) / np.sqrt(K) / s, "e2m1")
    return {
        "tab_words": p_tab[0],
        "tab_scales": p_tab[1],
        "wu_words": p_wu[0],
        "wu_scales": p_wu[1],
        "sm": (np.random.uniform(0.5, 2.0, R) * u[:, 0]).astype(np.float32),
        "wd": (n((R, N)) / np.sqrt(R) / u).astype(np.float32),
        "rT": (n((N, T))).astype(np.float32),
        "b": (0.3 * n(N)).astype(np.float32),
        "wgo": np.tile(np.random.uniform(0.5, 2.0, J), (128, 1)).astype(np.float32),
        "offs": striped(np.random.permutation(T)[:J]),
    }


def reference(tab_words, tab_scales, wu_words, wu_scales, sm, wd, rT, b, wgo, offs):
    idx = unstriped(offs)
    tab_ = unpack_weight(tab_words, tab_scales, "e4m3")[:, idx]
    wu_ = unpack_weight(wu_words, wu_scales, "e2m1")
    a = wu_.T @ tab_
    h = f64(sm)[:, None] * gelu(a)
    h_ = mxq(h, 0, "e4m3")
    wd_ = mxq(f64(wd), 0, "e4m3")
    y = wd_.T @ h_
    out = np.zeros((N, T))
    out[:, idx] = f64(wgo)[0] * (y + f64(rT)[:, idx] + f64(b)[:, None])
    return out

@@ -1,0 +1,164 @@
+from contextlib import ExitStack
+
+import concourse.mybir as mybir
+
+K, R, N, T, J = 512, 512, 512, 2048, 1024
+FLOPS = 2 * K * R * J + 2 * R * N * J
+
+F32 = mybir.dt.float32
+BF16 = mybir.dt.bfloat16
+I32 = mybir.dt.int32
+U32 = mybir.dt.uint32
+U16 = mybir.dt.uint16
+U8 = mybir.dt.uint8
+FP8X4 = mybir.dt.float8_e4m3fn_x4
+FP4X4 = mybir.dt.float4_e2m1fn_x4
+ACT = mybir.ActivationFunctionType
+ALU = mybir.AluOpType
+
+P = 128
+PACK = 4
+CH = 256
+NCH = J // CH
+NT = N // P
+
+
+def tile_list_modp_gelu_resb_kernel(
+    tc, tab_words, tab_scales, wu_words, wu_scales, sm, wd, rT, b, wgo, offs, out
+):
+    nc = tc.nc
+    with ExitStack() as ctx:
+        keep = ctx.enter_context(tc.tile_pool(name="keep", bufs=1))
+        ring = ctx.enter_context(tc.tile_pool(name="ring", bufs=4))
+        psum = ctx.enter_context(tc.psum_pool(name="psum", bufs=4))
+
+        offsets = keep.tile([P, J // 16], U16, name="offsets")
+        tab_w = keep.tile([P, T], I32, name="tab_w", align_bytes=64)
+        tab_s = keep.tile([P, T // 4], I32, name="tab_s", align_bytes=64)
+        wu_w_raw = keep.tile([P, R // 2], I32, name="wu_w_raw", align_bytes=64)
+        wu_s_raw = keep.tile([P, R // 4], I32, name="wu_s_raw", tag="staged", align_bytes=64)
+        wu_w = keep.tile([P, 2 * R], U8, name="wu_w", align_bytes=64)
+        wu_s = keep.tile([P, R], U8, name="wu_s", align_bytes=64)
+        v_w_first = keep.tile([P, CH], U32, name="v_w_first", align_bytes=64)
+        v_s = keep.tile([P, J], U8, name="v_s", align_bytes=64)
+        sm_sb = keep.tile([P, PACK], F32, name="sm_sb")
+        b_sb = keep.tile([P, NT], F32, name="b_sb")
+        wgo_sb = keep.tile([P, J], F32, name="wgo_sb")
+        wd_raw = keep.tile([P, PACK, N], F32, name="wd_raw")
+        wd_bf = keep.tile([P, N, PACK], BF16, name="wd_bf", align_bytes=64)
+        wd_w = keep.tile([P, N], U32, name="wd_w", align_bytes=64)
+        wd_s = keep.tile([P, N], U8, name="wd_s", align_bytes=64)
+        h_w = keep.tile([P, J], U32, name="h_w", align_bytes=64)
+        h_s = keep.tile([P, J], U8, name="h_s", align_bytes=64)
+        r_tab = [keep.tile([P, T], F32, name="r_tab%d" % t) for t in range(NT)]
+        r_pick = [keep.tile([P, J], F32, name="r_pick%d" % t) for t in range(NT)]
+        total = [keep.tile([P, J], F32, name="total%d" % t) for t in range(NT)]
+        window = [keep.tile([P, T], F32, name="window%d" % t) for t in range(NT)]
+        warm = keep.tile([P, 1], F32, name="warm")
+        warm_out = keep.tile([P, 1], F32, name="warm_out")
+
+        nc.vector.memset(wu_s_raw[:], 0)
+        nc.gpsimd.memset(tab_s[:], 0)
+        for t in range(NT):
+            nc.gpsimd.memset(window[t][:], 0.0)
+        nc.vector.memset(warm[:], 0.0)
+        nc.scalar.activation(warm_out[:], warm[:], ACT.Gelu_apprx_tanh)
+
+        nc.sync.dma_start(offsets[:], offs)
+        nc.sync.dma_start(wu_w_raw[:], wu_words[0].bitcast(I32))
+        for q in range(4):
+            nc.sync.dma_start(tab_s[32 * q : 32 * q + 4, :], tab_scales[0, 4 * q : 4 * q + 4, :].bitcast(I32))
+        nc.sync.dma_start(tab_w[:], tab_words[0].rearrange("p t i -> p (t i)").bitcast(I32))
+        for q in range(4):
+            nc.sync.dma_start(wu_s_raw[32 * q : 32 * q + 4, :], wu_scales[0, 4 * q : 4 * q + 4, :].bitcast(I32))
+        nc.sync.dma_start(sm_sb[:], sm.rearrange("(p t) -> p t", t=PACK))
+        nc.sync.dma_start(r_tab[0][:], rT[0:P, :])
+        nc.sync.dma_start(r_tab[1][:], rT[P : 2 * P, :])
+        nc.sync.dma_start(wd_raw[:], wd.rearrange("(p j) n -> p j n", j=PACK))
+        nc.sync.dma_start(r_tab[2][:], rT[2 * P : 3 * P, :])
+        with nc.allow_non_contiguous_dma(reason="one bias value a partition"):
+            nc.sync.dma_start(b_sb[:], b.rearrange("(t p) -> p t", p=P))
+        nc.sync.dma_start(r_tab[3][:], rT[3 * P : 4 * P, :])
+        nc.sync.dma_start(wgo_sb[:], wgo)
+
+        def listed(a, z):
+            return offsets[:, a // 16 : z // 16]
+
+        def hidden(c, words):
+            cols = slice(c * CH, (c + 1) * CH)
+            act = ring.tile([P, PACK, CH], F32, name="act")
+            for half in range(2):
+                bank = psum.tile([P, 2, CH], F32, name="bank_a")
+                for u in range(2):
+                    t = 2 * half + u
+                    nc.tensor.matmul_mx(
+                        out=bank[:, u, :],
+                        lhsT=wu_w[:, 2 * P * t : 2 * P * (t + 1)].bitcast(FP4X4),
+                        lhsT_scale=wu_s[:, P * t : P * (t + 1)],
+                        rhs=words.bitcast(FP8X4),
+                        rhs_scale=v_s[:, cols],
+                        start=True,
+                        stop=True,
+                    )
+                nc.scalar.activation(act[:, 2 * half : 2 * half + 2, :], bank[:], ACT.Gelu_apprx_tanh)
+            planes = ring.tile([P, PACK, CH], BF16, name="planes")
+            for t in range(PACK):
+                nc.scalar.activation(planes[:, t, :], act[:, t, :], ACT.Copy, scale=sm_sb[:, t : t + 1])
+            woven = ring.tile([P, CH, PACK], BF16, name="woven", align_bytes=64)
+            nc.scalar.copy(
+                woven[:].rearrange("p (c i) t -> p c t i", i=4),
+                planes[:].rearrange("p t (c i) -> p c t i", i=4),
+            )
+            nc.vector.quantize_mx(
+                out=h_w[:, cols].bitcast(FP8X4), scales=h_s[:, cols], in_=woven[:].rearrange("p n t -> p (n t)")
+            )
+
+        def quantise_wd():
+            nc.scalar.copy(wd_bf[:], wd_raw[:].rearrange("p j n -> p n j"))
+            nc.vector.quantize_mx(
+                out=wd_w[:].bitcast(FP8X4), scales=wd_s[:], in_=wd_bf[:].rearrange("p n j -> p (n j)")
+            )
+
+        def gather_residual(t):
+            nc.vector.tensor_copy(r_pick[t][:], r_tab[t][:].indirect(offsets[:]))
+
+        def place(t, half):
+            a, z = half * (J // 2), (half + 1) * (J // 2)
+            bank = psum.tile([P, J // 2], F32, name="bank_y")
+            nc.tensor.matmul_mx(
+                out=bank[:],
+                lhsT=wd_w[:, P * t : P * (t + 1)].bitcast(FP8X4),
+                lhsT_scale=wd_s[:, P * t : P * (t + 1)],
+                rhs=h_w[:, a:z].bitcast(FP8X4),
+                rhs_scale=h_s[:, a:z],
+                start=True,
+                stop=True,
+            )
+            nc.vector.scalar_tensor_tensor(
+                total[t][:, a:z], bank[:], b_sb[:, t : t + 1], r_pick[t][:, a:z], ALU.add, ALU.add
+            )
+            nc.vector.tensor_tensor(window[t][:].indirect(listed(a, z)), total[t][:, a:z], wgo_sb[:, a:z], ALU.mult)
+
+        nc.vector.tensor_copy(v_w_first[:], tab_w[:].bitcast(U32).indirect(listed(0, CH)))
+        nc.vector.tensor_copy(v_s[:], tab_s[:].bitcast(U8).indirect(offsets[:]))
+        nc.vector.tensor_copy(
+            wu_w[:].bitcast(U16).rearrange("p (t m) -> p t m", t=PACK),
+            wu_w_raw[:].bitcast(U16).rearrange("p (m t) -> p t m", t=PACK),
+        )
+        nc.vector.tensor_copy(
+            wu_s[:].rearrange("p (t m) -> p m t", t=PACK),
+            wu_s_raw[:].bitcast(U8).rearrange("p (m t) -> p m t", t=PACK),
+        )
+        v_w_rest = keep.tile([P, J - CH], U32, name="v_w_rest", tag="staged", align_bytes=64)
+        nc.vector.tensor_copy(v_w_rest[:], tab_w[:].bitcast(U32).indirect(listed(CH, J)))
+        hidden(0, v_w_first[:])
+        quantise_wd()
+        for c in range(1, NCH):
+            hidden(c, v_w_rest[:, (c - 1) * CH : c * CH])
+        for t in range(NT):
+            gather_residual(t)
+        for t in range(NT):
+            place(t, 0)
+        for t in range(NT):
+            place(t, 1)
+            nc.sync.dma_start(out[P * t : P * (t + 1), :], window[t][:])

@@ -1,6 +1,7 @@
 from contextlib import ExitStack
 
 import concourse.mybir as mybir
+from concourse.masks import make_identity
 
 K, R, N, T, J = 512, 512, 512, 2048, 1024
 FLOPS = 2 * K * R * J + 2 * R * N * J
@@ -30,7 +31,7 @@ def tile_list_modp_gelu_resb_kernel(
     with ExitStack() as ctx:
         keep = ctx.enter_context(tc.tile_pool(name="keep", bufs=1))
         ring = ctx.enter_context(tc.tile_pool(name="ring", bufs=4))
-        psum = ctx.enter_context(tc.psum_pool(name="psum", bufs=4))
+        psum = ctx.enter_context(tc.psum_pool(name="psum", bufs=2))
 
         offsets = keep.tile([P, J // 16], U16, name="offsets")
         tab_w = keep.tile([P, T], I32, name="tab_w", align_bytes=64)
@@ -44,24 +45,31 @@ def tile_list_modp_gelu_resb_kernel(
         sm_sb = keep.tile([P, PACK], F32, name="sm_sb")
         b_sb = keep.tile([P, NT], F32, name="b_sb")
         wgo_sb = keep.tile([P, J], F32, name="wgo_sb")
-        wd_raw = keep.tile([P, PACK, N], F32, name="wd_raw")
+        wd_raw = [keep.tile([P, PACK, N // 2], F32, name="wd_raw%d" % i) for i in range(2)]
         wd_bf = keep.tile([P, N, PACK], BF16, name="wd_bf", align_bytes=64)
-        wd_w = keep.tile([P, N], U32, name="wd_w", align_bytes=64)
+        wd_w = {}
         wd_s = keep.tile([P, N], U8, name="wd_s", align_bytes=64)
-        h_w = keep.tile([P, J], U32, name="h_w", align_bytes=64)
+        h_w = {}
         h_s = keep.tile([P, J], U8, name="h_s", align_bytes=64)
-        r_tab = [keep.tile([P, T], F32, name="r_tab%d" % t) for t in range(NT)]
+        r_tab = [keep.tile([P, T], F32, name="r_tab%d" % t, tag="r_tab%d" % t, align_bytes=64) for t in range(NT)]
         r_pick = [keep.tile([P, J], F32, name="r_pick%d" % t) for t in range(NT)]
-        total = [keep.tile([P, J], F32, name="total%d" % t) for t in range(NT)]
-        window = [keep.tile([P, T], F32, name="window%d" % t) for t in range(NT)]
+        total = {
+            (t, a): keep.tile([P, J // 2], F32, name="total%d_%d" % (t, a), tag="total%d%d" % (t, a // (J // 2)), align_bytes=64)
+            for t in range(NT)
+            for a in (0, J // 2)
+        }
+        window = {t: keep.tile([P, T], F32, name="window%d" % t) for t in range(1)}
         warm = keep.tile([P, 1], F32, name="warm")
         warm_out = keep.tile([P, 1], F32, name="warm_out")
 
+        ident = keep.tile([P, P], F32, name="ident")
+        nc.vector.memset(tab_s[:], 0)
         nc.vector.memset(wu_s_raw[:], 0)
-        nc.gpsimd.memset(tab_s[:], 0)
-        for t in range(NT):
-            nc.gpsimd.memset(window[t][:], 0.0)
         nc.vector.memset(warm[:], 0.0)
+        nc.vector.memset(ident[:], 0.0)
+        make_identity(nc, ident[:], nomemset=True)
+        for t in range(1):
+            nc.vector.memset(window[t][:], 0.0)
         nc.scalar.activation(warm_out[:], warm[:], ACT.Gelu_apprx_tanh)
 
         nc.sync.dma_start(offsets[:], offs)
@@ -69,26 +77,29 @@ def tile_list_modp_gelu_resb_kernel(
         for q in range(4):
             nc.sync.dma_start(tab_s[32 * q : 32 * q + 4, :], tab_scales[0, 4 * q : 4 * q + 4, :].bitcast(I32))
         nc.sync.dma_start(tab_w[:], tab_words[0].rearrange("p t i -> p (t i)").bitcast(I32))
+        wd_rows = wd.rearrange("(p j) n -> p j n", j=PACK)
+        nc.sync.dma_start(wd_raw[0][:], wd_rows[:, :, 0 : N // 2])
         for q in range(4):
             nc.sync.dma_start(wu_s_raw[32 * q : 32 * q + 4, :], wu_scales[0, 4 * q : 4 * q + 4, :].bitcast(I32))
-        nc.sync.dma_start(sm_sb[:], sm.rearrange("(p t) -> p t", t=PACK))
+        nc.scalar.dma_start(sm_sb[:], sm.rearrange("(p t) -> p t", t=PACK))
         nc.sync.dma_start(r_tab[0][:], rT[0:P, :])
         nc.sync.dma_start(r_tab[1][:], rT[P : 2 * P, :])
-        nc.sync.dma_start(wd_raw[:], wd.rearrange("(p j) n -> p j n", j=PACK))
+        nc.sync.dma_start(wd_raw[1][:], wd_rows[:, :, N // 2 : N])
         nc.sync.dma_start(r_tab[2][:], rT[2 * P : 3 * P, :])
+        nc.sync.dma_start(wgo_sb[:, 0 : J // 2], wgo[:, 0 : J // 2])
+        nc.sync.dma_start(r_tab[3][:], rT[3 * P : 4 * P, :])
         with nc.allow_non_contiguous_dma(reason="one bias value a partition"):
             nc.sync.dma_start(b_sb[:], b.rearrange("(t p) -> p t", p=P))
-        nc.sync.dma_start(r_tab[3][:], rT[3 * P : 4 * P, :])
-        nc.sync.dma_start(wgo_sb[:], wgo)
+        nc.sync.dma_start(wgo_sb[:, J // 2 : J], wgo[:, J // 2 : J])
 
         def listed(a, z):
             return offsets[:, a // 16 : z // 16]
 
-        def hidden(c, words):
+        def hidden(c, words, h_tag, woven_tag):
             cols = slice(c * CH, (c + 1) * CH)
-            act = ring.tile([P, PACK, CH], F32, name="act")
+            act = keep.tile([P, PACK, CH], F32, name="act%d" % c, tag="act%d" % c, align_bytes=64)
             for half in range(2):
-                bank = psum.tile([P, 2, CH], F32, name="bank_a")
+                bank = psum.tile([P, 2, CH], F32, name="bank_a", tag="bank_a")
                 for u in range(2):
                     t = 2 * half + u
                     nc.tensor.matmul_mx(
@@ -104,40 +115,80 @@ def tile_list_modp_gelu_resb_kernel(
             planes = ring.tile([P, PACK, CH], BF16, name="planes")
             for t in range(PACK):
                 nc.scalar.activation(planes[:, t, :], act[:, t, :], ACT.Copy, scale=sm_sb[:, t : t + 1])
-            woven = ring.tile([P, CH, PACK], BF16, name="woven", align_bytes=64)
+            woven = keep.tile([P, CH, PACK], BF16, name="woven%d" % c, tag=woven_tag, align_bytes=64)
             nc.scalar.copy(
                 woven[:].rearrange("p (c i) t -> p c t i", i=4),
                 planes[:].rearrange("p t (c i) -> p c t i", i=4),
             )
+            h_w[c] = keep.tile([P, CH], U32, name="h_w%d" % c, tag=h_tag, align_bytes=64)
             nc.vector.quantize_mx(
-                out=h_w[:, cols].bitcast(FP8X4), scales=h_s[:, cols], in_=woven[:].rearrange("p n t -> p (n t)")
+                out=h_w[c][:].bitcast(FP8X4), scales=h_s[:, cols], in_=woven[:].rearrange("p n t -> p (n t)")
             )
 
-        def quantise_wd():
-            nc.scalar.copy(wd_bf[:], wd_raw[:].rearrange("p j n -> p n j"))
+        def quantise_wd(i, tag):
+            wd_w[i] = keep.tile([P, N // 2], U32, name="wd_w%d" % i, tag=tag, align_bytes=64)
+            cols = slice(i * (N // 2), (i + 1) * (N // 2))
+            nc.scalar.copy(wd_bf[:, cols, :], wd_raw[i][:].rearrange("p j n -> p n j"))
             nc.vector.quantize_mx(
-                out=wd_w[:].bitcast(FP8X4), scales=wd_s[:], in_=wd_bf[:].rearrange("p n j -> p (n j)")
+                out=wd_w[i][:].bitcast(FP8X4),
+                scales=wd_s[:, cols],
+                in_=wd_bf[:, cols, :].rearrange("p n j -> p (n j)"),
             )
 
         def gather_residual(t):
             nc.vector.tensor_copy(r_pick[t][:], r_tab[t][:].indirect(offsets[:]))
 
-        def place(t, half):
-            a, z = half * (J // 2), (half + 1) * (J // 2)
-            bank = psum.tile([P, J // 2], F32, name="bank_y")
-            nc.tensor.matmul_mx(
-                out=bank[:],
-                lhsT=wd_w[:, P * t : P * (t + 1)].bitcast(FP8X4),
-                lhsT_scale=wd_s[:, P * t : P * (t + 1)],
-                rhs=h_w[:, a:z].bitcast(FP8X4),
-                rhs_scale=h_s[:, a:z],
-                start=True,
-                stop=True,
-            )
+        def add_up(t, a, z):
+            bank = psum.tile([P, z - a], F32, name="bank_y", tag="bank_s")
+            for x in range(a, z, CH):
+                nc.tensor.matmul_mx(
+                    out=bank[:, x - a : x - a + CH],
+                    lhsT=wd_w[t // 2][:, P * (t % 2) : P * (t % 2 + 1)].bitcast(FP8X4),
+                    lhsT_scale=wd_s[:, P * t : P * (t + 1)],
+                    rhs=h_w[x // CH][:].bitcast(FP8X4),
+                    rhs_scale=h_s[:, x : x + CH],
+                    start=True,
+                    stop=True,
+                )
             nc.vector.scalar_tensor_tensor(
-                total[t][:, a:z], bank[:], b_sb[:, t : t + 1], r_pick[t][:, a:z], ALU.add, ALU.add
+                total[t, a][:], bank[:], b_sb[:, t : t + 1], r_pick[t][:, a:z], ALU.add, ALU.add
             )
-            nc.vector.tensor_tensor(window[t][:].indirect(listed(a, z)), total[t][:, a:z], wgo_sb[:, a:z], ALU.mult)
+
+        def add_up_in_psum(t, a, ident):
+            r_turned = ring.tile([P, 4, P], F32, name="r_turned", bufs=1)
+            y_turned = ring.tile([P, 4, P], F32, name="y_turned", bufs=2)
+            blocks = [slice(a + P * i, a + P * (i + 1)) for i in range(4)]
+            bank_r = psum.tile([P, 4, P], F32, name="bank_r", bufs=2)
+            for i in range(4):
+                nc.tensor.transpose(bank_r[:, i, :], r_pick[t][:, blocks[i]], ident[:])
+            nc.scalar.copy(r_turned[:], bank_r[:])
+            bank_t = psum.tile([P, 4, P], F32, name="bank_t", bufs=1)
+            for i in range(4):
+                nc.tensor.matmul_mx(
+                    out=bank_t[:, i, :],
+                    lhsT=h_w[a // CH + i // 2][:, P * (i % 2) : P * (i % 2 + 1)].bitcast(FP8X4),
+                    lhsT_scale=h_s[:, blocks[i]],
+                    rhs=wd_w[t // 2][:, P * (t % 2) : P * (t % 2 + 1)].bitcast(FP8X4),
+                    rhs_scale=wd_s[:, P * t : P * (t + 1)],
+                    start=True,
+                    stop=True,
+                )
+            nc.scalar.copy(y_turned[:], bank_t[:])
+            bank_s = psum.tile([P, 4, P], F32, name="bank_s", tag="bank_s")
+            for i in range(4):
+                nc.tensor.matmul(bank_s[:, i, :], r_turned[:, i, :], ident[:], start=i == 0, stop=False, is_transpose=True)
+            for i in range(4):
+                nc.tensor.matmul(bank_s[:, i, :], y_turned[:, i, :], ident[:], start=False, stop=i == 3, is_transpose=True)
+            nc.scalar.activation(
+                total[t, a][:].rearrange("p (i j) -> p i j", i=4), bank_s[:], ACT.Identity, bias=b_sb[:, t : t + 1]
+            )
+
+        def place(t, a, z):
+            nc.vector.tensor_tensor(
+                window[t][:].indirect(listed(a, z)), total[t, a][:], wgo_sb[:, a:z], ALU.mult
+            )
+            if z == J:
+                nc.sync.dma_start(out[P * t : P * (t + 1), :], window[t][:])
 
         nc.vector.tensor_copy(v_w_first[:], tab_w[:].bitcast(U32).indirect(listed(0, CH)))
         nc.vector.tensor_copy(v_s[:], tab_s[:].bitcast(U8).indirect(offsets[:]))
@@ -146,19 +197,40 @@ def tile_list_modp_gelu_resb_kernel(
             wu_w_raw[:].bitcast(U16).rearrange("p (m t) -> p t m", t=PACK),
         )
         nc.vector.tensor_copy(
-            wu_s[:].rearrange("p (t m) -> p m t", t=PACK),
-            wu_s_raw[:].bitcast(U8).rearrange("p (m t) -> p m t", t=PACK),
+            wu_s[:].rearrange("p (t m) -> p t m", t=PACK),
+            wu_s_raw[:].bitcast(U8).rearrange("p (m t) -> p t m", t=PACK),
         )
         v_w_rest = keep.tile([P, J - CH], U32, name="v_w_rest", tag="staged", align_bytes=64)
         nc.vector.tensor_copy(v_w_rest[:], tab_w[:].bitcast(U32).indirect(listed(CH, J)))
-        hidden(0, v_w_first[:])
-        quantise_wd()
-        for c in range(1, NCH):
-            hidden(c, v_w_rest[:, (c - 1) * CH : c * CH])
-        for t in range(NT):
-            gather_residual(t)
-        for t in range(NT):
-            place(t, 0)
-        for t in range(NT):
-            place(t, 1)
-            nc.sync.dma_start(out[P * t : P * (t + 1), :], window[t][:])
+        gather_residual(0)
+        quantise_wd(0, "r_tab0")
+        gather_residual(1)
+        hidden(0, v_w_first[:], "r_tab1", "woven0")
+        hidden(1, v_w_rest[:, 0 * CH : 1 * CH], "h_w1", "woven1")
+        gather_residual(2)
+        quantise_wd(1, "r_tab2")
+        gather_residual(3)
+        window[1] = keep.tile([P, T], F32, name="window1", tag="r_tab3", align_bytes=64)
+        nc.gpsimd.memset(window[1][:], 0.0)
+        add_up(0, 0, 512)
+        place(0, 0, 512)
+        window[2] = keep.tile([P, T], F32, name="window2", tag="total00", align_bytes=64)
+        nc.gpsimd.memset(window[2][:], 0.0)
+        add_up_in_psum(1, 0, ident)
+        place(1, 0, 512)
+        window[3] = keep.tile([P, T], F32, name="window3", tag="total10", align_bytes=64)
+        nc.gpsimd.memset(window[3][:], 0.0)
+        hidden(2, v_w_rest[:, 1 * CH : 2 * CH], "h_w2", "woven2")
+        add_up_in_psum(2, 0, ident)
+        place(2, 0, 512)
+        hidden(3, v_w_rest[:, 2 * CH : 3 * CH], "h_w3", "woven3")
+        add_up_in_psum(3, 0, ident)
+        place(3, 0, 512)
+        add_up_in_psum(0, 512, ident)
+        place(0, 512, 1024)
+        add_up_in_psum(1, 512, ident)
+        place(1, 512, 1024)
+        add_up_in_psum(2, 512, ident)
+        place(2, 512, 1024)
+        add_up_in_psum(3, 512, ident)
+        place(3, 512, 1024)

@@ -19,9 +19,13 @@ ALU = mybir.AluOpType
 
 P = 128
 PACK = 4
-CH = 256
-NCH = J // CH
-NT = N // P
+QUADS = 4
+CHUNK = 256
+CHUNKS = J // CHUNK
+HALF = J // 2
+BLOCKS = HALF // P
+TILES = N // P
+WD_HALF = N // 2
 
 
 def tile_list_modp_gelu_resb_kernel(
@@ -30,78 +34,77 @@ def tile_list_modp_gelu_resb_kernel(
     nc = tc.nc
     with ExitStack() as ctx:
         keep = ctx.enter_context(tc.tile_pool(name="keep", bufs=1))
-        ring = ctx.enter_context(tc.tile_pool(name="ring", bufs=4))
+        ring = ctx.enter_context(tc.tile_pool(name="ring", bufs=CHUNKS))
         psum = ctx.enter_context(tc.psum_pool(name="psum", bufs=2))
 
         offsets = keep.tile([P, J // 16], U16, name="offsets")
         tab_w = keep.tile([P, T], I32, name="tab_w", align_bytes=64)
         tab_s = keep.tile([P, T // 4], I32, name="tab_s", align_bytes=64)
         wu_w_raw = keep.tile([P, R // 2], I32, name="wu_w_raw", align_bytes=64)
-        wu_s_raw = keep.tile([P, R // 4], I32, name="wu_s_raw", tag="staged", align_bytes=64)
+        wu_s_raw = keep.tile([P, R // 4], I32, name="wu_s_raw", tag="wu_s_raw", align_bytes=64)
         wu_w = keep.tile([P, 2 * R], U8, name="wu_w", align_bytes=64)
         wu_s = keep.tile([P, R], U8, name="wu_s", align_bytes=64)
-        v_w_first = keep.tile([P, CH], U32, name="v_w_first", align_bytes=64)
+        v_w_first = keep.tile([P, CHUNK], U32, name="v_w_first", align_bytes=64)
         v_s = keep.tile([P, J], U8, name="v_s", align_bytes=64)
         sm_sb = keep.tile([P, PACK], F32, name="sm_sb")
-        b_sb = keep.tile([P, NT], F32, name="b_sb")
+        b_sb = keep.tile([P, TILES], F32, name="b_sb")
         wgo_sb = keep.tile([P, J], F32, name="wgo_sb")
-        wd_raw = [keep.tile([P, PACK, N // 2], F32, name="wd_raw%d" % i) for i in range(2)]
+        wd_raw = [keep.tile([P, PACK, WD_HALF], F32, name="wd_raw%d" % i) for i in range(2)]
         wd_bf = keep.tile([P, N, PACK], BF16, name="wd_bf", align_bytes=64)
-        wd_w = {}
         wd_s = keep.tile([P, N], U8, name="wd_s", align_bytes=64)
-        h_w = {}
         h_s = keep.tile([P, J], U8, name="h_s", align_bytes=64)
-        r_tab = [keep.tile([P, T], F32, name="r_tab%d" % t, tag="r_tab%d" % t, align_bytes=64) for t in range(NT)]
-        r_pick = [keep.tile([P, J], F32, name="r_pick%d" % t) for t in range(NT)]
-        total = {
-            (t, a): keep.tile([P, J // 2], F32, name="total%d_%d" % (t, a), tag="total%d%d" % (t, a // (J // 2)), align_bytes=64)
-            for t in range(NT)
-            for a in (0, J // 2)
-        }
-        window = {t: keep.tile([P, T], F32, name="window%d" % t) for t in range(1)}
-        warm = keep.tile([P, 1], F32, name="warm")
-        warm_out = keep.tile([P, 1], F32, name="warm_out")
-
+        r_tab = [keep.tile([P, T], F32, name="r_tab%d" % t, tag="r_tab%d" % t, align_bytes=64) for t in range(TILES)]
+        r_pick = [keep.tile([P, J], F32, name="r_pick%d" % t) for t in range(TILES)]
+        total = [keep.tile([P, J], F32, name="total%d" % t) for t in range(TILES)]
+        window = [keep.tile([P, T], F32, name="window%d" % t) for t in range(2)]
+        zero = keep.tile([P, 1], F32, name="zero")
         ident = keep.tile([P, P], F32, name="ident")
+        wd_w = {}
+        h_w = {}
+
         nc.vector.memset(tab_s[:], 0)
         nc.vector.memset(wu_s_raw[:], 0)
-        nc.vector.memset(warm[:], 0.0)
-        nc.vector.memset(ident[:], 0.0)
+        nc.vector.memset(zero[:], 0.0)
+        for w in window:
+            nc.vector.memset(w[:], 0.0)
+        nc.scalar.activation(ident[:], zero[:].to_broadcast([P, P]), ACT.Gelu_apprx_tanh)
         make_identity(nc, ident[:], nomemset=True)
-        for t in range(1):
-            nc.vector.memset(window[t][:], 0.0)
-        nc.scalar.activation(warm_out[:], warm[:], ACT.Gelu_apprx_tanh)
 
+        def load_scale_rows(plane, rows):
+            for q in range(QUADS):
+                nc.sync.dma_start(plane[32 * q : 32 * q + 4, :], rows[0, 4 * q : 4 * q + 4, :].bitcast(I32))
+
+        def load_residual(t):
+            nc.sync.dma_start(r_tab[t][:], rT[P * t : P * (t + 1), :])
+
+        wd_rows = wd.rearrange("(p j) n -> p j n", j=PACK)
         nc.sync.dma_start(offsets[:], offs)
         nc.sync.dma_start(wu_w_raw[:], wu_words[0].bitcast(I32))
-        for q in range(4):
-            nc.sync.dma_start(tab_s[32 * q : 32 * q + 4, :], tab_scales[0, 4 * q : 4 * q + 4, :].bitcast(I32))
+        load_scale_rows(tab_s, tab_scales)
         nc.sync.dma_start(tab_w[:], tab_words[0].rearrange("p t i -> p (t i)").bitcast(I32))
-        wd_rows = wd.rearrange("(p j) n -> p j n", j=PACK)
-        nc.sync.dma_start(wd_raw[0][:], wd_rows[:, :, 0 : N // 2])
-        for q in range(4):
-            nc.sync.dma_start(wu_s_raw[32 * q : 32 * q + 4, :], wu_scales[0, 4 * q : 4 * q + 4, :].bitcast(I32))
+        nc.sync.dma_start(wd_raw[0][:], wd_rows[:, :, 0:WD_HALF])
+        load_scale_rows(wu_s_raw, wu_scales)
         nc.scalar.dma_start(sm_sb[:], sm.rearrange("(p t) -> p t", t=PACK))
-        nc.sync.dma_start(r_tab[0][:], rT[0:P, :])
-        nc.sync.dma_start(r_tab[1][:], rT[P : 2 * P, :])
-        nc.sync.dma_start(wd_raw[1][:], wd_rows[:, :, N // 2 : N])
-        nc.sync.dma_start(r_tab[2][:], rT[2 * P : 3 * P, :])
-        nc.sync.dma_start(wgo_sb[:, 0 : J // 2], wgo[:, 0 : J // 2])
-        nc.sync.dma_start(r_tab[3][:], rT[3 * P : 4 * P, :])
+        load_residual(0)
+        load_residual(1)
+        nc.sync.dma_start(wd_raw[1][:], wd_rows[:, :, WD_HALF:N])
+        load_residual(2)
+        nc.sync.dma_start(wgo_sb[:, 0:HALF], wgo[:, 0:HALF])
+        load_residual(3)
         with nc.allow_non_contiguous_dma(reason="one bias value a partition"):
             nc.sync.dma_start(b_sb[:], b.rearrange("(t p) -> p t", p=P))
-        nc.sync.dma_start(wgo_sb[:, J // 2 : J], wgo[:, J // 2 : J])
+        nc.sync.dma_start(wgo_sb[:, HALF:J], wgo[:, HALF:J])
 
         def listed(a, z):
             return offsets[:, a // 16 : z // 16]
 
-        def hidden(c, words, h_tag, woven_tag):
-            cols = slice(c * CH, (c + 1) * CH)
-            act = keep.tile([P, PACK, CH], F32, name="act%d" % c, tag="act%d" % c, align_bytes=64)
-            for half in range(2):
-                bank = psum.tile([P, 2, CH], F32, name="bank_a", tag="bank_a")
+        def hidden(c, words, h_tag):
+            cols = slice(c * CHUNK, (c + 1) * CHUNK)
+            act = keep.tile([P, PACK, CHUNK], F32, name="act%d" % c, align_bytes=64)
+            for pair in range(PACK // 2):
+                bank = psum.tile([P, 2, CHUNK], F32, name="bank_a")
                 for u in range(2):
-                    t = 2 * half + u
+                    t = 2 * pair + u
                     nc.tensor.matmul_mx(
                         out=bank[:, u, :],
                         lhsT=wu_w[:, 2 * P * t : 2 * P * (t + 1)].bitcast(FP4X4),
@@ -111,23 +114,23 @@ def tile_list_modp_gelu_resb_kernel(
                         start=True,
                         stop=True,
                     )
-                nc.scalar.activation(act[:, 2 * half : 2 * half + 2, :], bank[:], ACT.Gelu_apprx_tanh)
-            planes = ring.tile([P, PACK, CH], BF16, name="planes")
+                nc.scalar.activation(act[:, 2 * pair : 2 * pair + 2, :], bank[:], ACT.Gelu_apprx_tanh)
+            planes = ring.tile([P, PACK, CHUNK], BF16, name="planes")
             for t in range(PACK):
                 nc.scalar.activation(planes[:, t, :], act[:, t, :], ACT.Copy, scale=sm_sb[:, t : t + 1])
-            woven = keep.tile([P, CH, PACK], BF16, name="woven%d" % c, tag=woven_tag, align_bytes=64)
+            woven = keep.tile([P, CHUNK, PACK], BF16, name="woven%d" % c, tag="woven%d" % c, align_bytes=64)
             nc.scalar.copy(
                 woven[:].rearrange("p (c i) t -> p c t i", i=4),
                 planes[:].rearrange("p t (c i) -> p c t i", i=4),
             )
-            h_w[c] = keep.tile([P, CH], U32, name="h_w%d" % c, tag=h_tag, align_bytes=64)
+            h_w[c] = keep.tile([P, CHUNK], U32, name="h_w%d" % c, tag=h_tag, align_bytes=64)
             nc.vector.quantize_mx(
                 out=h_w[c][:].bitcast(FP8X4), scales=h_s[:, cols], in_=woven[:].rearrange("p n t -> p (n t)")
             )
 
         def quantise_wd(i, tag):
-            wd_w[i] = keep.tile([P, N // 2], U32, name="wd_w%d" % i, tag=tag, align_bytes=64)
-            cols = slice(i * (N // 2), (i + 1) * (N // 2))
+            wd_w[i] = keep.tile([P, WD_HALF], U32, name="wd_w%d" % i, tag=tag, align_bytes=64)
+            cols = slice(i * WD_HALF, (i + 1) * WD_HALF)
             nc.scalar.copy(wd_bf[:, cols, :], wd_raw[i][:].rearrange("p j n -> p n j"))
             nc.vector.quantize_mx(
                 out=wd_w[i][:].bitcast(FP8X4),
@@ -135,62 +138,67 @@ def tile_list_modp_gelu_resb_kernel(
                 in_=wd_bf[:, cols, :].rearrange("p n j -> p (n j)"),
             )
 
+        def wd_words(t):
+            return wd_w[t // 2][:, P * (t % 2) : P * (t % 2 + 1)].bitcast(FP8X4)
+
         def gather_residual(t):
             nc.vector.tensor_copy(r_pick[t][:], r_tab[t][:].indirect(offsets[:]))
 
-        def add_up(t, a, z):
-            bank = psum.tile([P, z - a], F32, name="bank_y", tag="bank_s")
-            for x in range(a, z, CH):
+        def sum_on_vector(t, a):
+            bank = psum.tile([P, HALF], F32, name="bank_y", tag="bank_y", bufs=1)
+            for x in range(a, a + HALF, CHUNK):
                 nc.tensor.matmul_mx(
-                    out=bank[:, x - a : x - a + CH],
-                    lhsT=wd_w[t // 2][:, P * (t % 2) : P * (t % 2 + 1)].bitcast(FP8X4),
+                    out=bank[:, x - a : x - a + CHUNK],
+                    lhsT=wd_words(t),
                     lhsT_scale=wd_s[:, P * t : P * (t + 1)],
-                    rhs=h_w[x // CH][:].bitcast(FP8X4),
-                    rhs_scale=h_s[:, x : x + CH],
+                    rhs=h_w[x // CHUNK][:].bitcast(FP8X4),
+                    rhs_scale=h_s[:, x : x + CHUNK],
                     start=True,
                     stop=True,
                 )
             nc.vector.scalar_tensor_tensor(
-                total[t, a][:], bank[:], b_sb[:, t : t + 1], r_pick[t][:, a:z], ALU.add, ALU.add
+                total[t][:, a : a + HALF], bank[:], b_sb[:, t : t + 1], r_pick[t][:, a : a + HALF], ALU.add, ALU.add
             )
 
-        def add_up_in_psum(t, a, ident):
-            r_turned = ring.tile([P, 4, P], F32, name="r_turned", bufs=1)
-            y_turned = ring.tile([P, 4, P], F32, name="y_turned", bufs=2)
-            blocks = [slice(a + P * i, a + P * (i + 1)) for i in range(4)]
-            bank_r = psum.tile([P, 4, P], F32, name="bank_r", bufs=2)
-            for i in range(4):
+        def sum_in_psum(t, a, sum_tag="bank_s", sum_bufs=2):
+            r_turned = ring.tile([P, BLOCKS, P], F32, name="r_turned", bufs=1)
+            y_turned = ring.tile([P, BLOCKS, P], F32, name="y_turned", bufs=2)
+            blocks = [slice(a + P * i, a + P * (i + 1)) for i in range(BLOCKS)]
+            bank_r = psum.tile([P, BLOCKS, P], F32, name="bank_r")
+            for i in range(BLOCKS):
                 nc.tensor.transpose(bank_r[:, i, :], r_pick[t][:, blocks[i]], ident[:])
             nc.scalar.copy(r_turned[:], bank_r[:])
-            bank_t = psum.tile([P, 4, P], F32, name="bank_t", bufs=1)
-            for i in range(4):
+            bank_t = psum.tile([P, BLOCKS, P], F32, name="bank_t", bufs=1)
+            for i in range(BLOCKS):
                 nc.tensor.matmul_mx(
                     out=bank_t[:, i, :],
-                    lhsT=h_w[a // CH + i // 2][:, P * (i % 2) : P * (i % 2 + 1)].bitcast(FP8X4),
+                    lhsT=h_w[a // CHUNK + i // 2][:, P * (i % 2) : P * (i % 2 + 1)].bitcast(FP8X4),
                     lhsT_scale=h_s[:, blocks[i]],
-                    rhs=wd_w[t // 2][:, P * (t % 2) : P * (t % 2 + 1)].bitcast(FP8X4),
+                    rhs=wd_words(t),
                     rhs_scale=wd_s[:, P * t : P * (t + 1)],
                     start=True,
                     stop=True,
                 )
             nc.scalar.copy(y_turned[:], bank_t[:])
-            bank_s = psum.tile([P, 4, P], F32, name="bank_s", tag="bank_s")
-            for i in range(4):
+            bank_s = psum.tile([P, BLOCKS, P], F32, name="sum_in_" + sum_tag, tag=sum_tag, bufs=sum_bufs)
+            for i in range(BLOCKS):
                 nc.tensor.matmul(bank_s[:, i, :], r_turned[:, i, :], ident[:], start=i == 0, stop=False, is_transpose=True)
-            for i in range(4):
-                nc.tensor.matmul(bank_s[:, i, :], y_turned[:, i, :], ident[:], start=False, stop=i == 3, is_transpose=True)
+            for i in range(BLOCKS):
+                last = i == BLOCKS - 1
+                nc.tensor.matmul(bank_s[:, i, :], y_turned[:, i, :], ident[:], start=False, stop=last, is_transpose=True)
             nc.scalar.activation(
-                total[t, a][:].rearrange("p (i j) -> p i j", i=4), bank_s[:], ACT.Identity, bias=b_sb[:, t : t + 1]
+                total[t][:, a : a + HALF].rearrange("p (i j) -> p i j", i=BLOCKS),
+                bank_s[:],
+                ACT.Identity,
+                bias=b_sb[:, t : t + 1],
             )
 
         def place(t, a, z):
-            nc.vector.tensor_tensor(
-                window[t][:].indirect(listed(a, z)), total[t, a][:], wgo_sb[:, a:z], ALU.mult
-            )
+            nc.vector.tensor_tensor(window[t][:].indirect(listed(a, z)), total[t][:, a:z], wgo_sb[:, a:z], ALU.mult)
             if z == J:
                 nc.sync.dma_start(out[P * t : P * (t + 1), :], window[t][:])
 
-        nc.vector.tensor_copy(v_w_first[:], tab_w[:].bitcast(U32).indirect(listed(0, CH)))
+        nc.vector.tensor_copy(v_w_first[:], tab_w[:].bitcast(U32).indirect(listed(0, CHUNK)))
         nc.vector.tensor_copy(v_s[:], tab_s[:].bitcast(U8).indirect(offsets[:]))
         nc.vector.tensor_copy(
             wu_w[:].bitcast(U16).rearrange("p (t m) -> p t m", t=PACK),
@@ -200,37 +208,36 @@ def tile_list_modp_gelu_resb_kernel(
             wu_s[:].rearrange("p (t m) -> p t m", t=PACK),
             wu_s_raw[:].bitcast(U8).rearrange("p (m t) -> p t m", t=PACK),
         )
-        v_w_rest = keep.tile([P, J - CH], U32, name="v_w_rest", tag="staged", align_bytes=64)
-        nc.vector.tensor_copy(v_w_rest[:], tab_w[:].bitcast(U32).indirect(listed(CH, J)))
+        v_w_rest = keep.tile([P, J - CHUNK], U32, name="v_w_rest", tag="wu_s_raw", align_bytes=64)
+        nc.vector.tensor_copy(v_w_rest[:], tab_w[:].bitcast(U32).indirect(listed(CHUNK, J)))
+
+        def rest_words(c):
+            return v_w_rest[:, (c - 1) * CHUNK : c * CHUNK]
+
         gather_residual(0)
         quantise_wd(0, "r_tab0")
         gather_residual(1)
-        hidden(0, v_w_first[:], "r_tab1", "woven0")
-        hidden(1, v_w_rest[:, 0 * CH : 1 * CH], "h_w1", "woven1")
+        hidden(0, v_w_first[:], "r_tab1")
+        hidden(1, rest_words(1), "h_w1")
         gather_residual(2)
         quantise_wd(1, "r_tab2")
         gather_residual(3)
-        window[1] = keep.tile([P, T], F32, name="window1", tag="r_tab3", align_bytes=64)
-        nc.gpsimd.memset(window[1][:], 0.0)
-        add_up(0, 0, 512)
-        place(0, 0, 512)
-        window[2] = keep.tile([P, T], F32, name="window2", tag="total00", align_bytes=64)
-        nc.gpsimd.memset(window[2][:], 0.0)
-        add_up_in_psum(1, 0, ident)
-        place(1, 0, 512)
-        window[3] = keep.tile([P, T], F32, name="window3", tag="total10", align_bytes=64)
-        nc.gpsimd.memset(window[3][:], 0.0)
-        hidden(2, v_w_rest[:, 1 * CH : 2 * CH], "h_w2", "woven2")
-        add_up_in_psum(2, 0, ident)
-        place(2, 0, 512)
-        hidden(3, v_w_rest[:, 2 * CH : 3 * CH], "h_w3", "woven3")
-        add_up_in_psum(3, 0, ident)
-        place(3, 0, 512)
-        add_up_in_psum(0, 512, ident)
-        place(0, 512, 1024)
-        add_up_in_psum(1, 512, ident)
-        place(1, 512, 1024)
-        add_up_in_psum(2, 512, ident)
-        place(2, 512, 1024)
-        add_up_in_psum(3, 512, ident)
-        place(3, 512, 1024)
+
+        sum_on_vector(0, 0)
+        place(0, 0, HALF)
+        sum_in_psum(1, 0, "bank_y", 1)
+        place(1, 0, HALF)
+        hidden(2, rest_words(2), "h_w2")
+        hidden(3, rest_words(3), "h_w3")
+        window.append(keep.tile([P, T], F32, name="window2", tag="woven3", align_bytes=64))
+        nc.vector.memset(window[2][:], 0.0)
+        sum_in_psum(2, 0)
+        place(2, 0, HALF)
+
+        for t in range(TILES - 1):
+            sum_in_psum(t, HALF)
+            place(t, HALF, J)
+        window.append(window[0])
+        sum_in_psum(TILES - 1, 0)
+        sum_in_psum(TILES - 1, HALF)
+        place(TILES - 1, 0, J)

@@ -34,33 +34,38 @@ def tile_list_modp_gelu_resb_kernel(
     nc = tc.nc
     with ExitStack() as ctx:
         keep = ctx.enter_context(tc.tile_pool(name="keep", bufs=1))
-        ring = ctx.enter_context(tc.tile_pool(name="ring", bufs=CHUNKS))
-        psum = ctx.enter_context(tc.psum_pool(name="psum", bufs=2))
+        psum = ctx.enter_context(tc.psum_pool(name="psum", bufs=1))
+
+        def sb(shape, dtype, name, tag=None):
+            return keep.tile(shape, dtype, name=name, tag=tag or name, align_bytes=64)
+
+        def bank(shape, name, tag):
+            return psum.tile(shape, F32, name=name, tag=tag)
 
         offsets = keep.tile([P, J // 16], U16, name="offsets")
-        tab_w = keep.tile([P, T], I32, name="tab_w", align_bytes=64)
-        tab_s = keep.tile([P, T // 4], I32, name="tab_s", align_bytes=64)
-        wu_w_raw = keep.tile([P, R // 2], I32, name="wu_w_raw", align_bytes=64)
-        wu_s_raw = keep.tile([P, R // 4], I32, name="wu_s_raw", tag="wu_s_raw", align_bytes=64)
-        wu_w = keep.tile([P, 2 * R], U8, name="wu_w", align_bytes=64)
-        wu_s = keep.tile([P, R], U8, name="wu_s", align_bytes=64)
-        v_w_first = keep.tile([P, CHUNK], U32, name="v_w_first", align_bytes=64)
-        v_s = keep.tile([P, J], U8, name="v_s", align_bytes=64)
-        sm_sb = keep.tile([P, PACK], F32, name="sm_sb")
-        b_sb = keep.tile([P, TILES], F32, name="b_sb")
-        wgo_sb = keep.tile([P, J], F32, name="wgo_sb")
-        wd_raw = [keep.tile([P, PACK, WD_HALF], F32, name="wd_raw%d" % i) for i in range(2)]
-        wd_bf = keep.tile([P, N, PACK], BF16, name="wd_bf", align_bytes=64)
-        wd_s = keep.tile([P, N], U8, name="wd_s", align_bytes=64)
-        h_s = keep.tile([P, J], U8, name="h_s", align_bytes=64)
-        r_tab = [keep.tile([P, T], F32, name="r_tab%d" % t, tag="r_tab%d" % t, align_bytes=64) for t in range(TILES)]
-        r_pick = [keep.tile([P, J], F32, name="r_pick%d" % t) for t in range(TILES)]
-        total = [keep.tile([P, J], F32, name="total%d" % t) for t in range(TILES)]
-        window = [keep.tile([P, T], F32, name="window%d" % t) for t in range(2)]
-        zero = keep.tile([P, 1], F32, name="zero")
-        ident = keep.tile([P, P], F32, name="ident")
-        wd_w = {}
-        h_w = {}
+        tab_w = sb([P, T], I32, "tab_w")
+        tab_s = sb([P, T // 4], I32, "tab_s")
+        wu_w_raw = sb([P, R // 2], I32, "wu_w_raw")
+        wu_s_raw = sb([P, R // 4], I32, "wu_s_raw")
+        wu_w = sb([P, 2 * R], U8, "wu_w")
+        wu_s = sb([P, R], U8, "wu_s")
+        v_w_first = sb([P, CHUNK], U32, "v_w_first")
+        v_s = sb([P, J], U8, "v_s")
+        sm_sb = sb([P, PACK], F32, "sm_sb")
+        b_sb = sb([P, TILES], F32, "b_sb")
+        wgo_sb = sb([P, J], F32, "wgo_sb")
+        wd_cols = [slice(0, P), slice(P, 2 * P), slice(2 * P, N)]
+        wd_raw = [sb([P, PACK, s.stop - s.start], F32, "wd_raw%d" % i) for i, s in enumerate(wd_cols)]
+        wd_w = sb([P, N], U32, "wd_w")
+        wd_s = sb([P, N], U8, "wd_s")
+        h_s = sb([P, J], U8, "h_s")
+        h_w = [sb([P, CHUNK], U32, "h_w%d" % c) for c in range(CHUNKS)]
+        r_tab = [sb([P, T], F32, "r_tab%d" % t) for t in range(TILES)]
+        total = [None] + [sb([P, J], F32, "total%d" % t) for t in range(1, TILES)]
+        window = [sb([P, T], F32, "window%d" % t) for t in range(2)]
+        zero = sb([P, 1], F32, "zero")
+        ident = sb([P, P], F32, "ident")
+        r_pick = {}
 
         nc.vector.memset(tab_s[:], 0)
         nc.vector.memset(wu_s_raw[:], 0)
@@ -79,113 +84,124 @@ def tile_list_modp_gelu_resb_kernel(
 
         wd_rows = wd.rearrange("(p j) n -> p j n", j=PACK)
         nc.sync.dma_start(offsets[:], offs)
+        nc.scalar.dma_start(sm_sb[:], sm.rearrange("(p t) -> p t", t=PACK))
         nc.sync.dma_start(wu_w_raw[:], wu_words[0].bitcast(I32))
         load_scale_rows(tab_s, tab_scales)
         nc.sync.dma_start(tab_w[:], tab_words[0].rearrange("p t i -> p (t i)").bitcast(I32))
-        nc.sync.dma_start(wd_raw[0][:], wd_rows[:, :, 0:WD_HALF])
         load_scale_rows(wu_s_raw, wu_scales)
-        nc.scalar.dma_start(sm_sb[:], sm.rearrange("(p t) -> p t", t=PACK))
+        nc.sync.dma_start(wd_raw[0][:], wd_rows[:, :, wd_cols[0]])
         load_residual(0)
         load_residual(1)
-        nc.sync.dma_start(wd_raw[1][:], wd_rows[:, :, WD_HALF:N])
-        load_residual(2)
-        nc.sync.dma_start(wgo_sb[:, 0:HALF], wgo[:, 0:HALF])
-        load_residual(3)
+        nc.sync.dma_start(wd_raw[1][:], wd_rows[:, :, wd_cols[1]])
         with nc.allow_non_contiguous_dma(reason="one bias value a partition"):
             nc.sync.dma_start(b_sb[:], b.rearrange("(t p) -> p t", p=P))
-        nc.sync.dma_start(wgo_sb[:, HALF:J], wgo[:, HALF:J])
+        load_residual(2)
+        nc.sync.dma_start(wgo_sb[:], wgo)
+        load_residual(3)
+        nc.sync.dma_start(wd_raw[2][:], wd_rows[:, :, wd_cols[2]])
 
         def listed(a, z):
             return offsets[:, a // 16 : z // 16]
 
-        def hidden(c, words, h_tag):
-            cols = slice(c * CHUNK, (c + 1) * CHUNK)
-            act = keep.tile([P, PACK, CHUNK], F32, name="act%d" % c, align_bytes=64)
+        def hidden(c, words):
+            scales = v_s[:, c * CHUNK : (c + 1) * CHUNK]
+            act = sb([P, PACK, CHUNK], F32, "act%d" % c)
             for pair in range(PACK // 2):
-                bank = psum.tile([P, 2, CHUNK], F32, name="bank_a")
+                a_bank = bank([P, 2, CHUNK], "a%d_%d" % (c, pair), "A%d" % (2 * (c % 2) + pair))
                 for u in range(2):
                     t = 2 * pair + u
                     nc.tensor.matmul_mx(
-                        out=bank[:, u, :],
+                        out=a_bank[:, u, :],
                         lhsT=wu_w[:, 2 * P * t : 2 * P * (t + 1)].bitcast(FP4X4),
                         lhsT_scale=wu_s[:, P * t : P * (t + 1)],
                         rhs=words.bitcast(FP8X4),
-                        rhs_scale=v_s[:, cols],
+                        rhs_scale=scales,
                         start=True,
                         stop=True,
                     )
-                nc.scalar.activation(act[:, 2 * pair : 2 * pair + 2, :], bank[:], ACT.Gelu_apprx_tanh)
-            planes = ring.tile([P, PACK, CHUNK], BF16, name="planes")
+                nc.scalar.activation(act[:, 2 * pair : 2 * pair + 2, :], a_bank[:], ACT.Gelu_apprx_tanh)
+            planes = sb([P, PACK, CHUNK], BF16, "planes%d" % c)
             for t in range(PACK):
                 nc.scalar.activation(planes[:, t, :], act[:, t, :], ACT.Copy, scale=sm_sb[:, t : t + 1])
-            woven = keep.tile([P, CHUNK, PACK], BF16, name="woven%d" % c, tag="woven%d" % c, align_bytes=64)
+            woven = sb([P, CHUNK, PACK], BF16, "woven%d" % c)
             nc.scalar.copy(
                 woven[:].rearrange("p (c i) t -> p c t i", i=4),
                 planes[:].rearrange("p t (c i) -> p c t i", i=4),
             )
-            h_w[c] = keep.tile([P, CHUNK], U32, name="h_w%d" % c, tag=h_tag, align_bytes=64)
+            return woven
+
+        def quantise_h(c, woven):
             nc.vector.quantize_mx(
-                out=h_w[c][:].bitcast(FP8X4), scales=h_s[:, cols], in_=woven[:].rearrange("p n t -> p (n t)")
+                out=h_w[c][:].bitcast(FP8X4),
+                scales=h_s[:, c * CHUNK : (c + 1) * CHUNK],
+                in_=woven[:].rearrange("p n t -> p (n t)"),
             )
 
         def quantise_wd(i, tag):
-            wd_w[i] = keep.tile([P, WD_HALF], U32, name="wd_w%d" % i, tag=tag, align_bytes=64)
-            cols = slice(i * WD_HALF, (i + 1) * WD_HALF)
-            nc.scalar.copy(wd_bf[:, cols, :], wd_raw[i][:].rearrange("p j n -> p n j"))
+            cols = wd_cols[i]
+            wd_bf = sb([P, cols.stop - cols.start, PACK], BF16, "wd_bf%d" % i, tag)
+            nc.scalar.copy(wd_bf[:], wd_raw[i][:].rearrange("p j n -> p n j"))
             nc.vector.quantize_mx(
-                out=wd_w[i][:].bitcast(FP8X4),
-                scales=wd_s[:, cols],
-                in_=wd_bf[:, cols, :].rearrange("p n j -> p (n j)"),
+                out=wd_w[:, cols].bitcast(FP8X4), scales=wd_s[:, cols], in_=wd_bf[:].rearrange("p n j -> p (n j)")
             )
 
         def wd_words(t):
-            return wd_w[t // 2][:, P * (t % 2) : P * (t % 2 + 1)].bitcast(FP8X4)
+            return wd_w[:, P * t : P * (t + 1)].bitcast(FP8X4)
 
         def gather_residual(t):
-            nc.vector.tensor_copy(r_pick[t][:], r_tab[t][:].indirect(offsets[:]))
+            whole = sb([P, J], F32, "r_pick%d" % t)
+            nc.vector.tensor_copy(whole[:], r_tab[t][:].indirect(offsets[:]))
+            r_pick[(t, 0)] = whole[:, 0:HALF]
+            r_pick[(t, 1)] = whole[:, HALF:J]
 
-        def sum_on_vector(t, a):
-            bank = psum.tile([P, HALF], F32, name="bank_y", tag="bank_y", bufs=1)
-            for x in range(a, a + HALF, CHUNK):
-                nc.tensor.matmul_mx(
-                    out=bank[:, x - a : x - a + CHUNK],
-                    lhsT=wd_words(t),
-                    lhsT_scale=wd_s[:, P * t : P * (t + 1)],
-                    rhs=h_w[x // CHUNK][:].bitcast(FP8X4),
-                    rhs_scale=h_s[:, x : x + CHUNK],
-                    start=True,
-                    stop=True,
-                )
-            nc.vector.scalar_tensor_tensor(
-                total[t][:, a : a + HALF], bank[:], b_sb[:, t : t + 1], r_pick[t][:, a : a + HALF], ALU.add, ALU.add
+        def gather_half(t, i, dst):
+            nc.vector.tensor_copy(dst, r_tab[t][:].indirect(listed(i * HALF, (i + 1) * HALF)))
+            r_pick[(t, i)] = dst
+
+        def first_product(c):
+            y_bank = bank([P, CHUNK], "y%d" % c, "Y%d" % (c % 2))
+            nc.tensor.matmul_mx(
+                out=y_bank[:],
+                lhsT=wd_words(0),
+                lhsT_scale=wd_s[:, 0:P],
+                rhs=h_w[c][:].bitcast(FP8X4),
+                rhs_scale=h_s[:, c * CHUNK : (c + 1) * CHUNK],
+                start=True,
+                stop=True,
             )
+            return y_bank
 
-        def sum_in_psum(t, a, sum_tag="bank_s", sum_bufs=2):
-            r_turned = ring.tile([P, BLOCKS, P], F32, name="r_turned", bufs=1)
-            y_turned = ring.tile([P, BLOCKS, P], F32, name="y_turned", bufs=2)
-            blocks = [slice(a + P * i, a + P * (i + 1)) for i in range(BLOCKS)]
-            bank_r = psum.tile([P, BLOCKS, P], F32, name="bank_r")
-            for i in range(BLOCKS):
-                nc.tensor.transpose(bank_r[:, i, :], r_pick[t][:, blocks[i]], ident[:])
+        def sum_on_vector(c, y_bank, dst):
+            picked = r_pick[(0, c // 2)][:, (c % 2) * CHUNK : (c % 2 + 1) * CHUNK]
+            nc.vector.scalar_tensor_tensor(dst, y_bank[:], b_sb[:, 0:1], picked, ALU.add, ALU.add)
+
+        def sum_in_psum(t, i):
+            u = 2 * t + i
+            a = i * HALF
+            r_turned = sb([P, BLOCKS, P], F32, "r_turned%d" % u, "act3" if i == 0 else "woven3")
+            y_turned = sb([P, BLOCKS, P], F32, "y_turned%d" % u, "y_turned%d" % i)
+            bank_r = bank([P, BLOCKS, P], "bank_r%d" % u, "A%d" % (2 + i))
+            for k in range(BLOCKS):
+                nc.tensor.transpose(bank_r[:, k, :], r_pick[(t, i)][:, P * k : P * (k + 1)], ident[:])
             nc.scalar.copy(r_turned[:], bank_r[:])
-            bank_t = psum.tile([P, BLOCKS, P], F32, name="bank_t", bufs=1)
-            for i in range(BLOCKS):
+            bank_t = bank([P, BLOCKS, P], "bank_t%d" % u, "Y0" if i == 0 else "A0")
+            for k in range(BLOCKS):
                 nc.tensor.matmul_mx(
-                    out=bank_t[:, i, :],
-                    lhsT=h_w[a // CHUNK + i // 2][:, P * (i % 2) : P * (i % 2 + 1)].bitcast(FP8X4),
-                    lhsT_scale=h_s[:, blocks[i]],
+                    out=bank_t[:, k, :],
+                    lhsT=h_w[a // CHUNK + k // 2][:, P * (k % 2) : P * (k % 2 + 1)].bitcast(FP8X4),
+                    lhsT_scale=h_s[:, a + P * k : a + P * (k + 1)],
                     rhs=wd_words(t),
                     rhs_scale=wd_s[:, P * t : P * (t + 1)],
                     start=True,
                     stop=True,
                 )
             nc.scalar.copy(y_turned[:], bank_t[:])
-            bank_s = psum.tile([P, BLOCKS, P], F32, name="sum_in_" + sum_tag, tag=sum_tag, bufs=sum_bufs)
-            for i in range(BLOCKS):
-                nc.tensor.matmul(bank_s[:, i, :], r_turned[:, i, :], ident[:], start=i == 0, stop=False, is_transpose=True)
-            for i in range(BLOCKS):
-                last = i == BLOCKS - 1
-                nc.tensor.matmul(bank_s[:, i, :], y_turned[:, i, :], ident[:], start=False, stop=last, is_transpose=True)
+            bank_s = bank([P, BLOCKS, P], "bank_s%d" % u, "S%d" % i)
+            for k in range(BLOCKS):
+                nc.tensor.matmul(bank_s[:, k, :], r_turned[:, k, :], ident[:], start=k == 0, stop=False, is_transpose=True)
+            for k in range(BLOCKS):
+                last = k == BLOCKS - 1
+                nc.tensor.matmul(bank_s[:, k, :], y_turned[:, k, :], ident[:], start=False, stop=last, is_transpose=True)
             nc.scalar.activation(
                 total[t][:, a : a + HALF].rearrange("p (i j) -> p i j", i=BLOCKS),
                 bank_s[:],
@@ -193,51 +209,50 @@ def tile_list_modp_gelu_resb_kernel(
                 bias=b_sb[:, t : t + 1],
             )
 
-        def place(t, a, z):
-            nc.vector.tensor_tensor(window[t][:].indirect(listed(a, z)), total[t][:, a:z], wgo_sb[:, a:z], ALU.mult)
+        def place(t, a, z, values):
+            win = window[t % 2]
+            nc.vector.tensor_tensor(win[:].indirect(listed(a, z)), values, wgo_sb[:, a:z], ALU.mult)
             if z == J:
-                nc.sync.dma_start(out[P * t : P * (t + 1), :], window[t][:])
+                nc.sync.dma_start(out[P * t : P * (t + 1), :], win[:])
 
-        nc.vector.tensor_copy(v_w_first[:], tab_w[:].bitcast(U32).indirect(listed(0, CHUNK)))
         nc.vector.tensor_copy(v_s[:], tab_s[:].bitcast(U8).indirect(offsets[:]))
         nc.vector.tensor_copy(
             wu_w[:].bitcast(U16).rearrange("p (t m) -> p t m", t=PACK),
             wu_w_raw[:].bitcast(U16).rearrange("p (m t) -> p t m", t=PACK),
         )
+        nc.vector.tensor_copy(v_w_first[:], tab_w[:].bitcast(U32).indirect(listed(0, CHUNK)))
         nc.vector.tensor_copy(
             wu_s[:].rearrange("p (t m) -> p t m", t=PACK),
             wu_s_raw[:].bitcast(U8).rearrange("p (m t) -> p t m", t=PACK),
         )
-        v_w_rest = keep.tile([P, J - CHUNK], U32, name="v_w_rest", tag="wu_s_raw", align_bytes=64)
+        v_w_rest = sb([P, J - CHUNK], U32, "v_w_rest", "wu_s_raw")
         nc.vector.tensor_copy(v_w_rest[:], tab_w[:].bitcast(U32).indirect(listed(CHUNK, J)))
 
-        def rest_words(c):
-            return v_w_rest[:, (c - 1) * CHUNK : c * CHUNK]
+        def words(c):
+            return v_w_first[:] if c == 0 else v_w_rest[:, (c - 1) * CHUNK : c * CHUNK]
 
         gather_residual(0)
-        quantise_wd(0, "r_tab0")
+        quantise_wd(0, None)
+        quantise_h(0, hidden(0, words(0)))
         gather_residual(1)
-        hidden(0, v_w_first[:], "r_tab1")
-        hidden(1, rest_words(1), "h_w1")
-        gather_residual(2)
-        quantise_wd(1, "r_tab2")
-        gather_residual(3)
+        y_bank = first_product(0)
+        gather_half(2, 0, sb([P, HALF], F32, "r_pick2a")[:])
+        pieces = [(2, 1), (3, 0), (3, 1)]
+        for c in range(1, CHUNKS):
+            quantise_h(c, hidden(c, words(c)))
+            held = sb([P, CHUNK + HALF], F32, "held%d" % c, "planes%d" % c)
+            sum_on_vector(c - 1, y_bank, held[:, 0:CHUNK])
+            y_bank = first_product(c)
+            gather_half(pieces[c - 1][0], pieces[c - 1][1], held[:, CHUNK : CHUNK + HALF])
+            place(0, (c - 1) * CHUNK, c * CHUNK, held[:, 0:CHUNK])
+            if c == 1:
+                quantise_wd(1, "act1")
+        last = sb([P, CHUNK], F32, "last")
+        sum_on_vector(CHUNKS - 1, y_bank, last[:])
+        place(0, J - CHUNK, J, last[:])
 
-        sum_on_vector(0, 0)
-        place(0, 0, HALF)
-        sum_in_psum(1, 0, "bank_y", 1)
-        place(1, 0, HALF)
-        hidden(2, rest_words(2), "h_w2")
-        hidden(3, rest_words(3), "h_w3")
-        window.append(keep.tile([P, T], F32, name="window2", tag="woven3", align_bytes=64))
-        nc.vector.memset(window[2][:], 0.0)
-        sum_in_psum(2, 0)
-        place(2, 0, HALF)
-
-        for t in range(TILES - 1):
-            sum_in_psum(t, HALF)
-            place(t, HALF, J)
-        window.append(window[0])
-        sum_in_psum(TILES - 1, 0)
-        sum_in_psum(TILES - 1, HALF)
-        place(TILES - 1, 0, J)
+        quantise_wd(2, "r_tab3")
+        for t in range(1, TILES):
+            sum_in_psum(t, 0)
+            sum_in_psum(t, 1)
+            place(t, 0, J, total[t][:])

@@ -56,10 +56,11 @@ def tile_list_modp_gelu_resb_kernel(
         wgo_sb = sb([P, J], F32, "wgo_sb")
         wd_cols = [slice(0, P), slice(P, 2 * P), slice(2 * P, N)]
         wd_raw = [sb([P, PACK, s.stop - s.start], F32, "wd_raw%d" % i) for i, s in enumerate(wd_cols)]
+        wd_src = [wd_raw[0][:], wd_raw[1][:], wd_raw[2][:, :, 0:P], wd_raw[2][:, :, P : 2 * P]]
         wd_w = sb([P, N], U32, "wd_w")
         wd_s = sb([P, N], U8, "wd_s")
         h_s = sb([P, J], U8, "h_s")
-        h_w = [sb([P, CHUNK], U32, "h_w%d" % c) for c in range(CHUNKS)]
+        h_w = sb([P, J], U32, "h_w")
         r_tab = [sb([P, T], F32, "r_tab%d" % t) for t in range(TILES)]
         total = [None] + [sb([P, J], F32, "total%d" % t) for t in range(1, TILES)]
         window = [sb([P, T], F32, "window%d" % t) for t in range(2)]
@@ -67,13 +68,15 @@ def tile_list_modp_gelu_resb_kernel(
         ident = sb([P, P], F32, "ident")
         r_pick = {}
 
-        nc.vector.memset(tab_s[:], 0)
-        nc.vector.memset(wu_s_raw[:], 0)
+        nc.gpsimd.memset(tab_s[:], 0)
+        nc.gpsimd.memset(wu_s_raw[:], 0)
+        make_identity(nc, ident[:])
+        nc.gpsimd.memset(window[1][:, HALF:T], 0.0)
         nc.vector.memset(zero[:], 0.0)
-        for w in window:
-            nc.vector.memset(w[:], 0.0)
-        nc.scalar.activation(ident[:], zero[:].to_broadcast([P, P]), ACT.Gelu_apprx_tanh)
-        make_identity(nc, ident[:], nomemset=True)
+        nc.vector.memset(window[0][:], 0.0)
+        nc.vector.memset(window[1][:, 0:HALF], 0.0)
+        no_bias = sb([P, 1], F32, "no_bias")
+        nc.scalar.activation(no_bias[:], zero[:], ACT.Gelu_apprx_tanh)
 
         def load_scale_rows(plane, rows):
             for q in range(QUADS):
@@ -92,18 +95,19 @@ def tile_list_modp_gelu_resb_kernel(
         nc.sync.dma_start(wd_raw[0][:], wd_rows[:, :, wd_cols[0]])
         load_residual(0)
         load_residual(1)
-        nc.sync.dma_start(wd_raw[1][:], wd_rows[:, :, wd_cols[1]])
+        load_residual(2)
+        load_residual(3)
         with nc.allow_non_contiguous_dma(reason="one bias value a partition"):
             nc.sync.dma_start(b_sb[:], b.rearrange("(t p) -> p t", p=P))
-        load_residual(2)
-        nc.sync.dma_start(wgo_sb[:], wgo)
-        load_residual(3)
+        nc.sync.dma_start(wgo_sb[:, 0:HALF], wgo[:, 0:HALF])
+        nc.sync.dma_start(wd_raw[1][:], wd_rows[:, :, wd_cols[1]])
+        nc.sync.dma_start(wgo_sb[:, HALF:J], wgo[:, HALF:J])
         nc.sync.dma_start(wd_raw[2][:], wd_rows[:, :, wd_cols[2]])
 
         def listed(a, z):
             return offsets[:, a // 16 : z // 16]
 
-        def hidden(c, words):
+        def hidden(c, words, woven):
             scales = v_s[:, c * CHUNK : (c + 1) * CHUNK]
             act = sb([P, PACK, CHUNK], F32, "act%d" % c)
             for pair in range(PACK // 2):
@@ -119,84 +123,78 @@ def tile_list_modp_gelu_resb_kernel(
                         start=True,
                         stop=True,
                     )
-                nc.scalar.activation(act[:, 2 * pair : 2 * pair + 2, :], a_bank[:], ACT.Gelu_apprx_tanh)
+                nc.scalar.activation(act[:, 2 * pair : 2 * pair + 2, :], a_bank[:], ACT.Gelu_apprx_tanh, bias=no_bias[:])
             planes = sb([P, PACK, CHUNK], BF16, "planes%d" % c)
             for t in range(PACK):
                 nc.scalar.activation(planes[:, t, :], act[:, t, :], ACT.Copy, scale=sm_sb[:, t : t + 1])
-            woven = sb([P, CHUNK, PACK], BF16, "woven%d" % c)
             nc.scalar.copy(
-                woven[:].rearrange("p (c i) t -> p c t i", i=4),
+                woven.rearrange("p (c i) t -> p c t i", i=4),
                 planes[:].rearrange("p t (c i) -> p c t i", i=4),
             )
-            return woven
 
-        def quantise_h(c, woven):
+        def quantise_h(a, z, woven):
             nc.vector.quantize_mx(
-                out=h_w[c][:].bitcast(FP8X4),
-                scales=h_s[:, c * CHUNK : (c + 1) * CHUNK],
-                in_=woven[:].rearrange("p n t -> p (n t)"),
+                out=h_w[:, a:z].bitcast(FP8X4), scales=h_s[:, a:z], in_=woven.rearrange("p n t -> p (n t)")
             )
 
-        def quantise_wd(i, tag):
-            cols = wd_cols[i]
-            wd_bf = sb([P, cols.stop - cols.start, PACK], BF16, "wd_bf%d" % i, tag)
-            nc.scalar.copy(wd_bf[:], wd_raw[i][:].rearrange("p j n -> p n j"))
+        def quantise_wd(i, flat):
+            cols = slice(P * i, P * (i + 1))
+            nc.scalar.copy(flat.rearrange("p (n j) -> p n j", j=PACK), wd_src[i].rearrange("p j n -> p n j"))
             nc.vector.quantize_mx(
-                out=wd_w[:, cols].bitcast(FP8X4), scales=wd_s[:, cols], in_=wd_bf[:].rearrange("p n j -> p (n j)")
+                out=wd_w[:, cols].bitcast(FP8X4), scales=wd_s[:, cols], in_=flat
             )
 
         def wd_words(t):
             return wd_w[:, P * t : P * (t + 1)].bitcast(FP8X4)
 
-        def gather_residual(t):
-            whole = sb([P, J], F32, "r_pick%d" % t)
-            nc.vector.tensor_copy(whole[:], r_tab[t][:].indirect(offsets[:]))
-            r_pick[(t, 0)] = whole[:, 0:HALF]
-            r_pick[(t, 1)] = whole[:, HALF:J]
+        def gather_residual(t, a, z, dst):
+            nc.vector.tensor_copy(dst, r_tab[t][:].indirect(listed(a, z)))
+            for c in range(a // CHUNK, z // CHUNK):
+                r_pick[(t, c)] = dst[:, c * CHUNK - a : (c + 1) * CHUNK - a]
 
-        def gather_half(t, i, dst):
-            nc.vector.tensor_copy(dst, r_tab[t][:].indirect(listed(i * HALF, (i + 1) * HALF)))
-            r_pick[(t, i)] = dst
+        def picked(t, a, width):
+            return r_pick[(t, a // CHUNK)][:, a % CHUNK : a % CHUNK + width]
 
-        def first_product(c):
-            y_bank = bank([P, CHUNK], "y%d" % c, "Y%d" % (c % 2))
+        def first_product(a, z, tag):
+            y_bank = bank([P, z - a], "y%d" % a, tag)
             nc.tensor.matmul_mx(
                 out=y_bank[:],
                 lhsT=wd_words(0),
                 lhsT_scale=wd_s[:, 0:P],
-                rhs=h_w[c][:].bitcast(FP8X4),
-                rhs_scale=h_s[:, c * CHUNK : (c + 1) * CHUNK],
+                rhs=h_w[:, a:z].bitcast(FP8X4),
+                rhs_scale=h_s[:, a:z],
                 start=True,
                 stop=True,
             )
             return y_bank
 
-        def sum_on_vector(c, y_bank, dst):
-            picked = r_pick[(0, c // 2)][:, (c % 2) * CHUNK : (c % 2 + 1) * CHUNK]
-            nc.vector.scalar_tensor_tensor(dst, y_bank[:], b_sb[:, 0:1], picked, ALU.add, ALU.add)
+        def sum_on_vector(a, z, y_bank, dst):
+            nc.vector.scalar_tensor_tensor(dst, y_bank[:], b_sb[:, 0:1], r_first[:, a:z], ALU.add, ALU.add)
 
-        def sum_in_psum(t, i):
+        def sum_in_psum(t, i, y_turned=None):
             u = 2 * t + i
             a = i * HALF
             r_turned = sb([P, BLOCKS, P], F32, "r_turned%d" % u, "act3" if i == 0 else "woven3")
-            y_turned = sb([P, BLOCKS, P], F32, "y_turned%d" % u, "y_turned%d" % i)
+            if y_turned is None:
+                y_turned = sb([P, BLOCKS, P], F32, "y_turned%d" % u, "y_turned%d" % i)[:]
             bank_r = bank([P, BLOCKS, P], "bank_r%d" % u, "A%d" % (2 + i))
             for k in range(BLOCKS):
-                nc.tensor.transpose(bank_r[:, k, :], r_pick[(t, i)][:, P * k : P * (k + 1)], ident[:])
+                nc.tensor.transpose(bank_r[:, k, :], picked(t, a + P * k, P), ident[:])
             nc.scalar.copy(r_turned[:], bank_r[:])
-            bank_t = bank([P, BLOCKS, P], "bank_t%d" % u, "Y0" if i == 0 else "A0")
+            pair = ["A1", "S0"] if i == 0 else ["A0", "S1"]
+            bank_t = bank([P, BLOCKS, P], "bank_t%d" % u, pair[(t + 1) % 2])
             for k in range(BLOCKS):
                 nc.tensor.matmul_mx(
                     out=bank_t[:, k, :],
-                    lhsT=h_w[a // CHUNK + k // 2][:, P * (k % 2) : P * (k % 2 + 1)].bitcast(FP8X4),
+                    lhsT=h_w[:, a + P * k : a + P * (k + 1)].bitcast(FP8X4),
                     lhsT_scale=h_s[:, a + P * k : a + P * (k + 1)],
                     rhs=wd_words(t),
                     rhs_scale=wd_s[:, P * t : P * (t + 1)],
                     start=True,
                     stop=True,
                 )
-            nc.scalar.copy(y_turned[:], bank_t[:])
-            bank_s = bank([P, BLOCKS, P], "bank_s%d" % u, "S%d" % i)
+            nc.scalar.copy(y_turned, bank_t[:])
+            bank_s = bank([P, BLOCKS, P], "bank_s%d" % u, pair[t % 2])
             for k in range(BLOCKS):
                 nc.tensor.matmul(bank_s[:, k, :], r_turned[:, k, :], ident[:], start=k == 0, stop=False, is_transpose=True)
             for k in range(BLOCKS):
@@ -231,28 +229,46 @@ def tile_list_modp_gelu_resb_kernel(
         def words(c):
             return v_w_first[:] if c == 0 else v_w_rest[:, (c - 1) * CHUNK : c * CHUNK]
 
-        gather_residual(0)
-        quantise_wd(0, None)
-        quantise_h(0, hidden(0, words(0)))
-        gather_residual(1)
-        y_bank = first_product(0)
-        gather_half(2, 0, sb([P, HALF], F32, "r_pick2a")[:])
-        pieces = [(2, 1), (3, 0), (3, 1)]
-        for c in range(1, CHUNKS):
-            quantise_h(c, hidden(c, words(c)))
-            held = sb([P, CHUNK + HALF], F32, "held%d" % c, "planes%d" % c)
-            sum_on_vector(c - 1, y_bank, held[:, 0:CHUNK])
-            y_bank = first_product(c)
-            gather_half(pieces[c - 1][0], pieces[c - 1][1], held[:, CHUNK : CHUNK + HALF])
-            place(0, (c - 1) * CHUNK, c * CHUNK, held[:, 0:CHUNK])
-            if c == 1:
-                quantise_wd(1, "act1")
+        r_first = sb([P, J], F32, "r_pick0")
+        gather_residual(0, 0, J, r_first[:])
+        quantise_wd(0, sb([P, P * PACK], BF16, "wd_bf0")[:])
+        woven = sb([P, HALF, PACK], BF16, "woven01")
+        hidden(0, words(0), woven[:, 0:CHUNK, :])
+        gather_residual(1, 0, J, sb([P, J], F32, "r_pick1")[:])
+        gather_residual(2, 0, J, sb([P, J], F32, "r_pick2")[:])
+        hidden(1, words(1), woven[:, CHUNK:HALF, :])
+        quantise_h(0, HALF, woven[:])
+        y_bank = first_product(0, HALF, "Y1")
+        held1 = sb([P, J], F32, "held1", "planes1")
+        gather_residual(3, 0, HALF, held1[:, HALF:J])
+        sum_on_vector(0, HALF, y_bank, held1[:, 0:HALF])
+        quantise_wd(1, sb([P, P * PACK], BF16, "wd_bf1", "act1")[:])
+        place(0, 0, HALF, held1[:, 0:HALF])
+
+        woven = sb([P, CHUNK, PACK], BF16, "woven2")
+        hidden(2, words(2), woven[:])
+        quantise_h(HALF, HALF + CHUNK, woven[:])
+        y_bank = first_product(HALF, HALF + CHUNK, "Y0")
+        gather_residual(3, HALF, J, sb([P, HALF], F32, "held2", "planes2")[:])
+
+        woven = sb([P, CHUNK, PACK], BF16, "woven3")
+        hidden(3, words(3), woven[:])
+        quantise_h(J - CHUNK, J, woven[:])
+        held3 = sb([P, 4 * CHUNK], F32, "held3", "planes3")
+        sum_on_vector(HALF, HALF + CHUNK, y_bank, held3[:, 0:CHUNK])
+        place(0, HALF, HALF + CHUNK, held3[:, 0:CHUNK])
+        y_bank = first_product(J - CHUNK, J, "Y0")
         last = sb([P, CHUNK], F32, "last")
-        sum_on_vector(CHUNKS - 1, y_bank, last[:])
+        sum_on_vector(J - CHUNK, J, y_bank, last[:])
+        quantise_wd(2, held3[:, CHUNK : 2 * CHUNK].bitcast(BF16))
         place(0, J - CHUNK, J, last[:])
 
-        quantise_wd(2, "r_tab3")
-        for t in range(1, TILES):
+        sum_in_psum(1, 0, held3[:, 2 * CHUNK : 4 * CHUNK].rearrange("p (k m) -> p k m", k=BLOCKS))
+        place(1, 0, HALF, total[1][:, 0:HALF])
+        quantise_wd(3, sb([P, P * PACK], BF16, "wd_bf3", "last")[:])
+        sum_in_psum(1, 1)
+        place(1, HALF, J, total[1][:, HALF:J])
+        for t in range(2, TILES):
             sum_in_psum(t, 0)
             sum_in_psum(t, 1)
             place(t, 0, J, total[t][:])

@@ -1,7 +1,6 @@
 from contextlib import ExitStack
 
 import concourse.mybir as mybir
-from concourse.masks import make_identity
 
 K, R, N, T, J = 512, 512, 512, 2048, 1024
 FLOPS = 2 * K * R * J + 2 * R * N * J
@@ -63,18 +62,18 @@ def tile_list_modp_gelu_resb_kernel(
         h_w = sb([P, J], U32, "h_w")
         r_tab = [sb([P, T], F32, "r_tab%d" % t) for t in range(TILES)]
         total = [None] + [sb([P, J], F32, "total%d" % t) for t in range(1, TILES)]
-        window = [sb([P, T], F32, "window%d" % t) for t in range(2)]
+        window = [sb([P, T], F32, "window0")]
         zero = sb([P, 1], F32, "zero")
         ident = sb([P, P], F32, "ident")
         r_pick = {}
 
         nc.gpsimd.memset(tab_s[:], 0)
-        nc.gpsimd.memset(wu_s_raw[:], 0)
-        make_identity(nc, ident[:])
-        nc.gpsimd.memset(window[1][:, HALF:T], 0.0)
+        distance = sb([P, P], I32, "distance")
+        nc.gpsimd.iota(distance[:], [[-1, P]], base=0, channel_multiplier=1)
         nc.vector.memset(zero[:], 0.0)
+        nc.vector.memset(wu_s_raw[:], 0)
         nc.vector.memset(window[0][:], 0.0)
-        nc.vector.memset(window[1][:, 0:HALF], 0.0)
+        nc.vector.tensor_single_scalar(ident[:], distance[:], 0.0, ALU.is_equal)
         no_bias = sb([P, 1], F32, "no_bias")
         nc.scalar.activation(no_bias[:], zero[:], ACT.Gelu_apprx_tanh)
 
@@ -95,13 +94,13 @@ def tile_list_modp_gelu_resb_kernel(
         nc.sync.dma_start(wd_raw[0][:], wd_rows[:, :, wd_cols[0]])
         load_residual(0)
         load_residual(1)
-        load_residual(2)
-        load_residual(3)
         with nc.allow_non_contiguous_dma(reason="one bias value a partition"):
             nc.sync.dma_start(b_sb[:], b.rearrange("(t p) -> p t", p=P))
+        load_residual(2)
         nc.sync.dma_start(wgo_sb[:, 0:HALF], wgo[:, 0:HALF])
-        nc.sync.dma_start(wd_raw[1][:], wd_rows[:, :, wd_cols[1]])
         nc.sync.dma_start(wgo_sb[:, HALF:J], wgo[:, HALF:J])
+        load_residual(3)
+        nc.sync.dma_start(wd_raw[1][:], wd_rows[:, :, wd_cols[1]])
         nc.sync.dma_start(wd_raw[2][:], wd_rows[:, :, wd_cols[2]])
 
         def listed(a, z):
@@ -229,43 +228,43 @@ def tile_list_modp_gelu_resb_kernel(
         def words(c):
             return v_w_first[:] if c == 0 else v_w_rest[:, (c - 1) * CHUNK : c * CHUNK]
 
+        def step(c):
+            woven = sb([P, CHUNK, PACK], BF16, "woven%d" % c)
+            hidden(c, words(c), woven[:])
+            quantise_h(c * CHUNK, (c + 1) * CHUNK, woven[:])
+
         r_first = sb([P, J], F32, "r_pick0")
         gather_residual(0, 0, J, r_first[:])
         quantise_wd(0, sb([P, P * PACK], BF16, "wd_bf0")[:])
-        woven = sb([P, HALF, PACK], BF16, "woven01")
-        hidden(0, words(0), woven[:, 0:CHUNK, :])
+        step(0)
+        window.append(sb([P, T], F32, "window1", "r_tab0"))
+        nc.vector.memset(window[1][:], 0.0)
         gather_residual(1, 0, J, sb([P, J], F32, "r_pick1")[:])
-        gather_residual(2, 0, J, sb([P, J], F32, "r_pick2")[:])
-        hidden(1, words(1), woven[:, CHUNK:HALF, :])
-        quantise_h(0, HALF, woven[:])
-        y_bank = first_product(0, HALF, "Y1")
-        held1 = sb([P, J], F32, "held1", "planes1")
-        gather_residual(3, 0, HALF, held1[:, HALF:J])
-        sum_on_vector(0, HALF, y_bank, held1[:, 0:HALF])
-        quantise_wd(1, sb([P, P * PACK], BF16, "wd_bf1", "act1")[:])
-        place(0, 0, HALF, held1[:, 0:HALF])
+        y_bank = first_product(0, CHUNK, "Y0")
+        for c in range(1, CHUNKS - 1):
+            step(c)
+            held = sb([P, CHUNK + HALF], F32, "held%d" % c, "planes%d" % c)
+            sum_on_vector((c - 1) * CHUNK, c * CHUNK, y_bank, held[:, 0:CHUNK])
+            y_bank = first_product(c * CHUNK, (c + 1) * CHUNK, "Y%d" % (c % 2))
+            gather_residual(2, (c - 1) * HALF, c * HALF, held[:, CHUNK : CHUNK + HALF])
+            place(0, (c - 1) * CHUNK, c * CHUNK, held[:, 0:CHUNK])
 
-        woven = sb([P, CHUNK, PACK], BF16, "woven2")
-        hidden(2, words(2), woven[:])
-        quantise_h(HALF, HALF + CHUNK, woven[:])
-        y_bank = first_product(HALF, HALF + CHUNK, "Y0")
-        gather_residual(3, HALF, J, sb([P, HALF], F32, "held2", "planes2")[:])
-
-        woven = sb([P, CHUNK, PACK], BF16, "woven3")
-        hidden(3, words(3), woven[:])
-        quantise_h(J - CHUNK, J, woven[:])
-        held3 = sb([P, 4 * CHUNK], F32, "held3", "planes3")
+        step(3)
+        held3 = sb([P, 10 * CHUNK], F32, "held3", "planes3")
         sum_on_vector(HALF, HALF + CHUNK, y_bank, held3[:, 0:CHUNK])
+        gather_residual(3, 0, HALF, held3[:, 5 * CHUNK : 7 * CHUNK])
+        quantise_wd(1, held3[:, 4 * CHUNK : 5 * CHUNK].bitcast(BF16))
         place(0, HALF, HALF + CHUNK, held3[:, 0:CHUNK])
         y_bank = first_product(J - CHUNK, J, "Y0")
         last = sb([P, CHUNK], F32, "last")
         sum_on_vector(J - CHUNK, J, y_bank, last[:])
+        gather_residual(3, HALF, J, held3[:, 7 * CHUNK : 9 * CHUNK])
         quantise_wd(2, held3[:, CHUNK : 2 * CHUNK].bitcast(BF16))
         place(0, J - CHUNK, J, last[:])
 
         sum_in_psum(1, 0, held3[:, 2 * CHUNK : 4 * CHUNK].rearrange("p (k m) -> p k m", k=BLOCKS))
         place(1, 0, HALF, total[1][:, 0:HALF])
-        quantise_wd(3, sb([P, P * PACK], BF16, "wd_bf3", "last")[:])
+        quantise_wd(3, held3[:, 9 * CHUNK : 10 * CHUNK].bitcast(BF16))
         sum_in_psum(1, 1)
         place(1, HALF, J, total[1][:, HALF:J])
         for t in range(2, TILES):

@@ -25,6 +25,7 @@ HALF = J // 2
 BLOCKS = HALF // P
 TILES = N // P
 WD_HALF = N // 2
+SUM_BYTES = 4 * CHUNK
 
 
 def tile_list_modp_gelu_resb_kernel(
@@ -33,6 +34,7 @@ def tile_list_modp_gelu_resb_kernel(
     nc = tc.nc
     with ExitStack() as ctx:
         keep = ctx.enter_context(tc.tile_pool(name="keep", bufs=1))
+        shared = ctx.enter_context(tc.tile_pool(name="shared", bufs=1))
         psum = ctx.enter_context(tc.psum_pool(name="psum", bufs=1))
 
         def sb(shape, dtype, name, tag=None):
@@ -48,34 +50,32 @@ def tile_list_modp_gelu_resb_kernel(
         wu_s_raw = sb([P, R // 4], I32, "wu_s_raw")
         wu_w = sb([P, 2 * R], U8, "wu_w")
         wu_s = sb([P, R], U8, "wu_s")
-        v_w_first = sb([P, CHUNK], U32, "v_w_first")
-        v_s = sb([P, J], U8, "v_s")
         sm_sb = sb([P, PACK], F32, "sm_sb")
         b_sb = sb([P, TILES], F32, "b_sb")
-        wgo_sb = sb([P, J], F32, "wgo_sb")
+        wgo_all = sb([P, J], F32, "wgo_all")
         wd_cols = [slice(0, P), slice(P, 2 * P), slice(2 * P, N)]
         wd_raw = [sb([P, PACK, s.stop - s.start], F32, "wd_raw%d" % i) for i, s in enumerate(wd_cols)]
-        wd_src = [wd_raw[0][:], wd_raw[1][:], wd_raw[2][:, :, 0:P], wd_raw[2][:, :, P : 2 * P]]
-        wd_w = sb([P, N], U32, "wd_w")
-        wd_s = sb([P, N], U8, "wd_s")
-        h_s = sb([P, J], U8, "h_s")
+        h_s = {}
         h_w = sb([P, J], U32, "h_w")
         r_tab = [sb([P, T], F32, "r_tab%d" % t) for t in range(TILES)]
-        total = [None] + [sb([P, J], F32, "total%d" % t) for t in range(1, TILES)]
-        window = [sb([P, T], F32, "window0")]
+        window = [sb([P, T], F32, "window%d" % i) for i in range(2)]
         zero = sb([P, 1], F32, "zero")
         ident = sb([P, P], F32, "ident")
-        r_pick = {}
 
         nc.gpsimd.memset(tab_s[:], 0)
-        distance = sb([P, P], I32, "distance")
-        nc.gpsimd.iota(distance[:], [[-1, P]], base=0, channel_multiplier=1)
+        nc.gpsimd.memset(wu_s_raw[:], 0)
+        distance = sb([P, P], F32, "distance")
+        nc.gpsimd.iota(distance[:], [[-1, P]], base=0, channel_multiplier=1, allow_small_or_imprecise_dtypes=True)
         nc.vector.memset(zero[:], 0.0)
-        nc.vector.memset(wu_s_raw[:], 0)
-        nc.vector.memset(window[0][:], 0.0)
-        nc.vector.tensor_single_scalar(ident[:], distance[:], 0.0, ALU.is_equal)
+        one = sb([P, 1], F32, "one")
+        nc.gpsimd.memset(one[:], 1.0)
+        nc.vector.memset(window[0][:].bitcast(I32), 0)
+        nc.vector.memset(window[1][:].bitcast(I32), 0)
         no_bias = sb([P, 1], F32, "no_bias")
         nc.scalar.activation(no_bias[:], zero[:], ACT.Gelu_apprx_tanh)
+        apart = sb([P, P], F32, "apart")
+        nc.scalar.activation(apart[:], distance[:], ACT.Abs, bias=no_bias[:])
+        nc.scalar.activation(ident[:], apart[:], ACT.Relu, bias=one[:], scale=-1.0)
 
         def load_scale_rows(plane, rows):
             for q in range(QUADS):
@@ -92,27 +92,31 @@ def tile_list_modp_gelu_resb_kernel(
         nc.sync.dma_start(tab_w[:], tab_words[0].rearrange("p t i -> p (t i)").bitcast(I32))
         load_scale_rows(wu_s_raw, wu_scales)
         nc.sync.dma_start(wd_raw[0][:], wd_rows[:, :, wd_cols[0]])
-        load_residual(0)
-        load_residual(1)
+        nc.sync.dma_start(wd_raw[1][:], wd_rows[:, :, wd_cols[1]])
+        load_residual(2)
+        load_residual(3)
         with nc.allow_non_contiguous_dma(reason="one bias value a partition"):
             nc.sync.dma_start(b_sb[:], b.rearrange("(t p) -> p t", p=P))
-        load_residual(2)
-        nc.sync.dma_start(wgo_sb[:, 0:HALF], wgo[:, 0:HALF])
-        nc.sync.dma_start(wgo_sb[:, HALF:J], wgo[:, HALF:J])
-        load_residual(3)
-        nc.sync.dma_start(wd_raw[1][:], wd_rows[:, :, wd_cols[1]])
+        load_residual(0)
+        load_residual(1)
+        nc.sync.dma_start(wgo_all[:, 0:CHUNK], wgo[:, 0:CHUNK])
+        nc.sync.dma_start(wgo_all[:, CHUNK:HALF], wgo[:, CHUNK:HALF])
+        nc.sync.dma_start(wgo_all[:, HALF:J], wgo[:, HALF:J])
         nc.sync.dma_start(wd_raw[2][:], wd_rows[:, :, wd_cols[2]])
 
         def listed(a, z):
             return offsets[:, a // 16 : z // 16]
 
-        def hidden(c, words, woven):
-            scales = v_s[:, c * CHUNK : (c + 1) * CHUNK]
-            act = sb([P, PACK, CHUNK], F32, "act%d" % c)
-            for pair in range(PACK // 2):
-                a_bank = bank([P, 2, CHUNK], "a%d_%d" % (c, pair), "A%d" % (2 * (c % 2) + pair))
-                for u in range(2):
-                    t = 2 * pair + u
+        def gather_words(a, z, dst):
+            nc.vector.tensor_copy(dst, tab_w[:].bitcast(U32).indirect(listed(a, z)))
+
+        def activated(a, words, scales, act, tags):
+            width = words.shape[1]
+            per_bank = PACK // len(tags)
+            for i, tag in enumerate(tags):
+                a_bank = bank([P, per_bank, width], "a%d_%d" % (a, i), tag)
+                for u in range(per_bank):
+                    t = per_bank * i + u
                     nc.tensor.matmul_mx(
                         out=a_bank[:, u, :],
                         lhsT=wu_w[:, 2 * P * t : 2 * P * (t + 1)].bitcast(FP4X4),
@@ -122,152 +126,187 @@ def tile_list_modp_gelu_resb_kernel(
                         start=True,
                         stop=True,
                     )
-                nc.scalar.activation(act[:, 2 * pair : 2 * pair + 2, :], a_bank[:], ACT.Gelu_apprx_tanh, bias=no_bias[:])
-            planes = sb([P, PACK, CHUNK], BF16, "planes%d" % c)
+                planes = slice(per_bank * i, per_bank * (i + 1))
+                nc.scalar.activation(act[:, planes, :], a_bank[:], ACT.Gelu_apprx_tanh, bias=no_bias[:])
+
+        def placed(shape, dtype, name, offset):
+            return shared.tile(shape, dtype, name=name, offset=offset, align_bytes=64)
+
+        def quantise_h(c, woven, plane):
+            h_s[c] = plane
+            nc.vector.quantize_mx(
+                out=h_w[:, c * CHUNK : (c + 1) * CHUNK].bitcast(FP8X4),
+                scales=h_s[c][:],
+                in_=woven[:].rearrange("p n t -> p (n t)"),
+            )
+
+        def hidden(c, words, scales):
+            if c > 0:
+                act = placed([P, PACK, CHUNK], F32, "act%d" % c, 7 * SUM_BYTES)
+            else:
+                act = sb([P, PACK, CHUNK], F32, "act%d" % c)
+            activated(c * CHUNK, words, scales, act, ["A%d" % (2 * (c % 2) + pair) for pair in range(2)])
+            if c == CHUNKS - 1:
+                planes = shared.tile([P, PACK, CHUNK], BF16, name="planes_last", offset=2 * SUM_BYTES, align_bytes=64)
+            elif c == 0:
+                planes = placed([P, PACK, CHUNK], BF16, "planes0", 10 * SUM_BYTES)
+            else:
+                planes = sb([P, PACK, CHUNK], BF16, "planes%d" % c)
             for t in range(PACK):
                 nc.scalar.activation(planes[:, t, :], act[:, t, :], ACT.Copy, scale=sm_sb[:, t : t + 1])
+            woven = sb([P, CHUNK, PACK], BF16, "woven%d" % c)
             nc.scalar.copy(
-                woven.rearrange("p (c i) t -> p c t i", i=4),
+                woven[:].rearrange("p (c i) t -> p c t i", i=4),
                 planes[:].rearrange("p t (c i) -> p c t i", i=4),
             )
+            return woven
 
-        def quantise_h(a, z, woven):
+        wd_w = {}
+        wd_s = sb([P, N], U8, "wd_s")
+
+        def quantise_wd(i, flat, codes):
             nc.vector.quantize_mx(
-                out=h_w[:, a:z].bitcast(FP8X4), scales=h_s[:, a:z], in_=woven.rearrange("p n t -> p (n t)")
+                out=codes.bitcast(FP8X4), scales=wd_s[:, WD_HALF * i : WD_HALF * (i + 1)], in_=flat
             )
+            for e in range(2):
+                wd_w[2 * i + e] = codes[:, P * e : P * (e + 1)].bitcast(FP8X4)
 
-        def quantise_wd(i, flat):
-            cols = slice(P * i, P * (i + 1))
-            nc.scalar.copy(flat.rearrange("p (n j) -> p n j", j=PACK), wd_src[i].rearrange("p j n -> p n j"))
-            nc.vector.quantize_mx(
-                out=wd_w[:, cols].bitcast(FP8X4), scales=wd_s[:, cols], in_=flat
-            )
+        def place(t, a, z, values):
+            win = window[t % 2]
+            nc.vector.tensor_tensor(win[:].indirect(listed(a, z)), values, wgo_all[:, a:z], ALU.mult)
+            if z == J:
+                nc.sync.dma_start(out[P * t : P * (t + 1), :], win[:])
 
-        def wd_words(t):
-            return wd_w[:, P * t : P * (t + 1)].bitcast(FP8X4)
-
-        def gather_residual(t, a, z, dst):
-            nc.vector.tensor_copy(dst, r_tab[t][:].indirect(listed(a, z)))
+        def product(t, a, z, y, tag):
+            y_bank = bank([P, z - a], "y%d_%d" % (t, a), tag)
             for c in range(a // CHUNK, z // CHUNK):
-                r_pick[(t, c)] = dst[:, c * CHUNK - a : (c + 1) * CHUNK - a]
+                nc.tensor.matmul_mx(
+                    out=y_bank[:, c * CHUNK - a : (c + 1) * CHUNK - a],
+                    lhsT=wd_w[t],
+                    lhsT_scale=wd_s[:, P * t : P * (t + 1)],
+                    rhs=h_w[:, c * CHUNK : (c + 1) * CHUNK].bitcast(FP8X4),
+                    rhs_scale=h_s[c][:],
+                    start=True,
+                    stop=True,
+                )
+            nc.scalar.activation(y, y_bank[:], ACT.Identity, bias=b_sb[:, t : t + 1])
 
-        def picked(t, a, width):
-            return r_pick[(t, a // CHUNK)][:, a % CHUNK : a % CHUNK + width]
+        def add_residual(t, a, z, y, total):
+            nc.vector.tensor_tensor(total, r_tab[t][:].indirect(listed(a, z)), y, ALU.add)
 
-        def first_product(a, z, tag):
-            y_bank = bank([P, z - a], "y%d" % a, tag)
-            nc.tensor.matmul_mx(
-                out=y_bank[:],
-                lhsT=wd_words(0),
-                lhsT_scale=wd_s[:, 0:P],
-                rhs=h_w[:, a:z].bitcast(FP8X4),
-                rhs_scale=h_s[:, a:z],
-                start=True,
-                stop=True,
-            )
-            return y_bank
-
-        def sum_on_vector(a, z, y_bank, dst):
-            nc.vector.scalar_tensor_tensor(dst, y_bank[:], b_sb[:, 0:1], r_first[:, a:z], ALU.add, ALU.add)
-
-        def sum_in_psum(t, i, y_turned=None):
+        def late_half(t, i, picked, total):
             u = 2 * t + i
             a = i * HALF
-            r_turned = sb([P, BLOCKS, P], F32, "r_turned%d" % u, "act3" if i == 0 else "woven3")
-            if y_turned is None:
-                y_turned = sb([P, BLOCKS, P], F32, "y_turned%d" % u, "y_turned%d" % i)[:]
-            bank_r = bank([P, BLOCKS, P], "bank_r%d" % u, "A%d" % (2 + i))
+            bank_r = bank([P, BLOCKS, P], "bank_r%d" % u, "Y0" if i == 0 else "A3")
             for k in range(BLOCKS):
-                nc.tensor.transpose(bank_r[:, k, :], picked(t, a + P * k, P), ident[:])
+                nc.tensor.transpose(bank_r[:, k, :], picked[:, P * k : P * (k + 1)], ident[:])
+            r_turned = sb([P, BLOCKS, P], F32, "r_turned%d" % u, "turned%d" % i)
             nc.scalar.copy(r_turned[:], bank_r[:])
-            pair = ["A1", "S0"] if i == 0 else ["A0", "S1"]
-            bank_t = bank([P, BLOCKS, P], "bank_t%d" % u, pair[(t + 1) % 2])
+            bank_t = bank([P, BLOCKS, P], "bank_t%d" % u, "A%d" % i)
             for k in range(BLOCKS):
                 nc.tensor.matmul_mx(
                     out=bank_t[:, k, :],
                     lhsT=h_w[:, a + P * k : a + P * (k + 1)].bitcast(FP8X4),
-                    lhsT_scale=h_s[:, a + P * k : a + P * (k + 1)],
-                    rhs=wd_words(t),
+                    lhsT_scale=h_s[2 * i + k // 2][:, P * (k % 2) : P * (k % 2 + 1)],
+                    rhs=wd_w[t],
                     rhs_scale=wd_s[:, P * t : P * (t + 1)],
                     start=True,
                     stop=True,
                 )
-            nc.scalar.copy(y_turned, bank_t[:])
-            bank_s = bank([P, BLOCKS, P], "bank_s%d" % u, pair[t % 2])
+            y_turned = sb([P, BLOCKS, P], F32, "y_turned%d" % u)
+            nc.scalar.copy(y_turned[:], bank_t[:])
+            bank_s = bank([P, BLOCKS, P], "bank_s%d" % u, "S%d" % i)
             for k in range(BLOCKS):
                 nc.tensor.matmul(bank_s[:, k, :], r_turned[:, k, :], ident[:], start=k == 0, stop=False, is_transpose=True)
             for k in range(BLOCKS):
                 last = k == BLOCKS - 1
                 nc.tensor.matmul(bank_s[:, k, :], y_turned[:, k, :], ident[:], start=False, stop=last, is_transpose=True)
             nc.scalar.activation(
-                total[t][:, a : a + HALF].rearrange("p (i j) -> p i j", i=BLOCKS),
-                bank_s[:],
-                ACT.Identity,
-                bias=b_sb[:, t : t + 1],
+                total.rearrange("p (i j) -> p i j", i=BLOCKS), bank_s[:], ACT.Identity, bias=b_sb[:, t : t + 1]
             )
 
-        def place(t, a, z, values):
-            win = window[t % 2]
-            nc.vector.tensor_tensor(win[:].indirect(listed(a, z)), values, wgo_sb[:, a:z], ALU.mult)
-            if z == J:
-                nc.sync.dma_start(out[P * t : P * (t + 1), :], win[:])
-
-        nc.vector.tensor_copy(v_s[:], tab_s[:].bitcast(U8).indirect(offsets[:]))
         nc.vector.tensor_copy(
             wu_w[:].bitcast(U16).rearrange("p (t m) -> p t m", t=PACK),
             wu_w_raw[:].bitcast(U16).rearrange("p (m t) -> p t m", t=PACK),
         )
-        nc.vector.tensor_copy(v_w_first[:], tab_w[:].bitcast(U32).indirect(listed(0, CHUNK)))
+        v_s0 = sb([P, CHUNK], U8, "v_s0")
+        nc.vector.tensor_copy(v_s0[:], tab_s[:].bitcast(U8).indirect(listed(0, CHUNK)))
+        v_w0 = sb([P, CHUNK], U32, "v_w0")
+        gather_words(0, CHUNK, v_w0[:])
         nc.vector.tensor_copy(
             wu_s[:].rearrange("p (t m) -> p t m", t=PACK),
             wu_s_raw[:].bitcast(U8).rearrange("p (m t) -> p t m", t=PACK),
         )
-        v_w_rest = sb([P, J - CHUNK], U32, "v_w_rest", "wu_s_raw")
-        nc.vector.tensor_copy(v_w_rest[:], tab_w[:].bitcast(U32).indirect(listed(CHUNK, J)))
+        v_s = sb([P, J - CHUNK], U8, "v_s", "wu_s_raw")
+        nc.vector.tensor_copy(v_s[:], tab_s[:].bitcast(U8).indirect(listed(CHUNK, J)))
+        wd_bf = sb([P, WD_HALF, PACK], BF16, "wd_bf0")
+        nc.scalar.copy(wd_bf[:, 0:P, :], wd_raw[0][:].rearrange("p j n -> p n j"))
+        v_w = sb([P, J - CHUNK], U32, "v_w", "wd_raw0")
+        nc.vector.tensor_copy(wd_bf[:, P : 2 * P, :], wd_raw[1][:].rearrange("p j n -> p n j"))
+        gather_words(CHUNK, J, v_w[:])
+        quantise_wd(0, wd_bf[:].rearrange("p n j -> p (n j)"), sb([P, WD_HALF], U32, "wd_w0")[:])
 
-        def words(c):
-            return v_w_first[:] if c == 0 else v_w_rest[:, (c - 1) * CHUNK : c * CHUNK]
+        picked = {}
 
-        def step(c):
-            woven = sb([P, CHUNK, PACK], BF16, "woven%d" % c)
-            hidden(c, words(c), woven[:])
-            quantise_h(c * CHUNK, (c + 1) * CHUNK, woven[:])
+        def gather_residual(t, a, z, dst):
+            nc.vector.tensor_copy(dst, r_tab[t][:].indirect(listed(a, z)))
+            for i in range(a // HALF, z // HALF):
+                picked[(t, i)] = dst[:, i * HALF - a : (i + 1) * HALF - a]
 
-        r_first = sb([P, J], F32, "r_pick0")
-        gather_residual(0, 0, J, r_first[:])
-        quantise_wd(0, sb([P, P * PACK], BF16, "wd_bf0")[:])
-        step(0)
-        window.append(sb([P, T], F32, "window1", "r_tab0"))
-        nc.vector.memset(window[1][:], 0.0)
-        gather_residual(1, 0, J, sb([P, J], F32, "r_pick1")[:])
-        y_bank = first_product(0, CHUNK, "Y0")
-        for c in range(1, CHUNKS - 1):
-            step(c)
-            held = sb([P, CHUNK + HALF], F32, "held%d" % c, "planes%d" % c)
-            sum_on_vector((c - 1) * CHUNK, c * CHUNK, y_bank, held[:, 0:CHUNK])
-            y_bank = first_product(c * CHUNK, (c + 1) * CHUNK, "Y%d" % (c % 2))
-            gather_residual(2, (c - 1) * HALF, c * HALF, held[:, CHUNK : CHUNK + HALF])
-            place(0, (c - 1) * CHUNK, c * CHUNK, held[:, 0:CHUNK])
+        def later(c):
+            rest = slice((c - 1) * CHUNK, c * CHUNK)
+            return hidden(c, v_w[:, rest], v_s[:, rest])
 
-        step(3)
-        held3 = sb([P, 10 * CHUNK], F32, "held3", "planes3")
-        sum_on_vector(HALF, HALF + CHUNK, y_bank, held3[:, 0:CHUNK])
-        gather_residual(3, 0, HALF, held3[:, 5 * CHUNK : 7 * CHUNK])
-        quantise_wd(1, held3[:, 4 * CHUNK : 5 * CHUNK].bitcast(BF16))
-        place(0, HALF, HALF + CHUNK, held3[:, 0:CHUNK])
-        y_bank = first_product(J - CHUNK, J, "Y0")
-        last = sb([P, CHUNK], F32, "last")
-        sum_on_vector(J - CHUNK, J, y_bank, last[:])
-        gather_residual(3, HALF, J, held3[:, 7 * CHUNK : 9 * CHUNK])
-        quantise_wd(2, held3[:, CHUNK : 2 * CHUNK].bitcast(BF16))
-        place(0, J - CHUNK, J, last[:])
+        def both_tiles(c, bank_tags, total):
+            a, z = c * CHUNK, (c + 1) * CHUNK
+            y = sb([P, 2, CHUNK], F32, "y_%d" % c)
+            for t in range(2):
+                product(t, a, z, y[:, t, :], bank_tags[t])
+                add_residual(t, a, z, y[:, t, :], total[t])
+            for t in range(2):
+                place(t, a, z, total[t])
 
-        sum_in_psum(1, 0, held3[:, 2 * CHUNK : 4 * CHUNK].rearrange("p (k m) -> p k m", k=BLOCKS))
-        place(1, 0, HALF, total[1][:, 0:HALF])
-        quantise_wd(3, held3[:, 9 * CHUNK : 10 * CHUNK].bitcast(BF16))
-        sum_in_psum(1, 1)
-        place(1, HALF, J, total[1][:, HALF:J])
+        gather_residual(2, 0, HALF, sb([P, HALF], F32, "picked2_0")[:])
+        quantise_h(0, hidden(0, v_w0[:], v_s0[:]), sb([P, CHUNK], U8, "h_s0"))
+        gather_residual(2, HALF, J, placed([P, HALF], F32, "picked2_1", 11 * SUM_BYTES)[:])
+        gather_residual(3, 0, J, sb([P, J], F32, "picked3")[:])
+        quantise_h(1, later(1), sb([P, CHUNK], U8, "h_s1"))
+        both_tiles(
+            0,
+            ["A2", "A3"],
+            [sb([P, CHUNK], F32, "total0_0")[:], placed([P, CHUNK], F32, "total1_0", SUM_BYTES // 2)[:]],
+        )
+        quantise_h(2, later(2), sb([P, CHUNK], U8, "h_s2", "total0_0"))
+        both_tiles(
+            1,
+            ["A0", "A1"],
+            [placed([P, CHUNK], F32, "total0_1", SUM_BYTES)[:], placed([P, CHUNK], F32, "total1_1", 0)[:]],
+        )
+
+        woven = later(3)
+        y = sb([P, CHUNK], F32, "y0_2")
+        product(0, HALF, HALF + CHUNK, y[:], "A2")
+        total = placed([P, CHUNK], F32, "total0_2", 3 * SUM_BYTES // 2)
+        add_residual(0, HALF, HALF + CHUNK, y[:], total[:])
+        quantise_h(3, woven, placed([P, CHUNK], U8, "h_s3", 0))
+        place(0, HALF, HALF + CHUNK, total[:])
+        y = sb([P, CHUNK], F32, "y0_3")
+        product(0, J - CHUNK, J, y[:], "Y0")
+        total = sb([P, CHUNK], F32, "total0_3")
+        add_residual(0, J - CHUNK, J, y[:], total[:])
+        wd_bf1 = placed([P, WD_HALF, PACK], BF16, "wd_bf1", 3 * SUM_BYTES)
+        nc.scalar.copy(wd_bf1[:], wd_raw[2][:].rearrange("p j n -> p n j"))
+        codes = sb([P, WD_HALF], U32, "wd_w1")
+        quantise_wd(1, wd_bf1[:].rearrange("p n j -> p (n j)"), codes[:])
+        place(0, J - CHUNK, J, total[:])
+        y = sb([P, HALF], F32, "y1_23")
+        product(1, HALF, J, y[:], "A3")
+        total = sb([P, HALF], F32, "total1_23", "y0_3")
+        add_residual(1, HALF, J, y[:], total[:])
+        place(1, HALF, J, total[:])
+
         for t in range(2, TILES):
-            sum_in_psum(t, 0)
-            sum_in_psum(t, 1)
-            place(t, 0, J, total[t][:])
+            total = sb([P, J], F32, "late_total%d" % t)
+            for i in range(2):
+                late_half(t, i, picked[(t, i)], total[:, HALF * i : HALF * (i + 1)])
+            place(t, 0, J, total[:])

@@ -62,20 +62,25 @@ def tile_list_modp_gelu_resb_kernel(
         zero = sb([P, 1], F32, "zero")
         ident = sb([P, P], F32, "ident")
 
-        nc.gpsimd.memset(tab_s[:], 0)
-        nc.gpsimd.memset(wu_s_raw[:], 0)
+        nc.vector.memset(tab_s[:], 0)
         distance = sb([P, P], F32, "distance")
-        nc.gpsimd.iota(distance[:], [[-1, P]], base=0, channel_multiplier=1, allow_small_or_imprecise_dtypes=True)
+        nc.gpsimd.iota(
+            distance[:, 0:1], [[0, 1]], base=0, channel_multiplier=-1, allow_small_or_imprecise_dtypes=True
+        )
         nc.vector.memset(zero[:], 0.0)
-        one = sb([P, 1], F32, "one")
-        nc.gpsimd.memset(one[:], 1.0)
+        nc.vector.memset(wu_s_raw[:], 0)
         nc.vector.memset(window[0][:].bitcast(I32), 0)
         nc.vector.memset(window[1][:].bitcast(I32), 0)
         no_bias = sb([P, 1], F32, "no_bias")
         nc.scalar.activation(no_bias[:], zero[:], ACT.Gelu_apprx_tanh)
+        for step in range(7):
+            width = 2**step
+            nc.scalar.activation(distance[:, width : 2 * width], distance[:, 0:width], ACT.Copy, bias=float(width))
         apart = sb([P, P], F32, "apart")
         nc.scalar.activation(apart[:], distance[:], ACT.Abs, bias=no_bias[:])
-        nc.scalar.activation(ident[:], apart[:], ACT.Relu, bias=one[:], scale=-1.0)
+        near = sb([P, P], F32, "near")
+        nc.scalar.activation(near[:], apart[:], ACT.Copy, bias=1.0, scale=-1.0)
+        nc.scalar.activation(ident[:], near[:], ACT.Relu, bias=no_bias[:])
 
         def load_scale_rows(plane, rows):
             for q in range(QUADS):
@@ -86,7 +91,7 @@ def tile_list_modp_gelu_resb_kernel(
 
         wd_rows = wd.rearrange("(p j) n -> p j n", j=PACK)
         nc.sync.dma_start(offsets[:], offs)
-        nc.scalar.dma_start(sm_sb[:], sm.rearrange("(p t) -> p t", t=PACK))
+        nc.sync.dma_start(sm_sb[:], sm.rearrange("(p t) -> p t", t=PACK))
         nc.sync.dma_start(wu_w_raw[:], wu_words[0].bitcast(I32))
         load_scale_rows(tab_s, tab_scales)
         nc.sync.dma_start(tab_w[:], tab_words[0].rearrange("p t i -> p (t i)").bitcast(I32))

@@ -26,6 +26,7 @@ BLOCKS = HALF // P
 TILES = N // P
 WD_HALF = N // 2
 SUM_BYTES = 4 * CHUNK
+FIRST = 768
 
 
 def tile_list_modp_gelu_resb_kernel(
@@ -146,20 +147,20 @@ def tile_list_modp_gelu_resb_kernel(
             )
 
         def hidden(c, words, scales):
-            if c > 0:
-                act = placed([P, PACK, CHUNK], F32, "act%d" % c, 7 * SUM_BYTES)
-            else:
-                act = sb([P, PACK, CHUNK], F32, "act%d" % c)
+            act = placed([P, PACK, CHUNK], F32, "act%d" % c, 7 * SUM_BYTES)
             activated(c * CHUNK, words, scales, act, ["A%d" % (2 * (c % 2) + pair) for pair in range(2)])
             if c == CHUNKS - 1:
                 planes = shared.tile([P, PACK, CHUNK], BF16, name="planes_last", offset=2 * SUM_BYTES, align_bytes=64)
             elif c == 0:
-                planes = placed([P, PACK, CHUNK], BF16, "planes0", 10 * SUM_BYTES)
+                planes = placed([P, PACK, CHUNK], BF16, "planes0", 11 * SUM_BYTES)
             else:
-                planes = sb([P, PACK, CHUNK], BF16, "planes%d" % c)
+                planes = placed([P, PACK, CHUNK], BF16, "planes%d" % c, (16 + 2 * c) * SUM_BYTES)
             for t in range(PACK):
                 nc.scalar.activation(planes[:, t, :], act[:, t, :], ACT.Copy, scale=sm_sb[:, t : t + 1])
-            woven = sb([P, CHUNK, PACK], BF16, "woven%d" % c)
+            if c == CHUNKS - 1:
+                woven = placed([P, CHUNK, PACK], BF16, "woven_last", 15 * SUM_BYTES)
+            else:
+                woven = sb([P, CHUNK, PACK], BF16, "woven%d" % c)
             nc.scalar.copy(
                 woven[:].rearrange("p (c i) t -> p c t i", i=4),
                 planes[:].rearrange("p t (c i) -> p c t i", i=4),
@@ -204,8 +205,8 @@ def tile_list_modp_gelu_resb_kernel(
             a = i * HALF
             bank_r = bank([P, BLOCKS, P], "bank_r%d" % u, "Y0" if i == 0 else "A3")
             for k in range(BLOCKS):
-                nc.tensor.transpose(bank_r[:, k, :], picked[:, P * k : P * (k + 1)], ident[:])
-            r_turned = sb([P, BLOCKS, P], F32, "r_turned%d" % u, "turned%d" % i)
+                nc.tensor.transpose(bank_r[:, k, :], picked[k], ident[:])
+            r_turned = placed([P, BLOCKS, P], F32, "r_turned%d" % u, (14 + 2 * i) * SUM_BYTES)
             nc.scalar.copy(r_turned[:], bank_r[:])
             bank_t = bank([P, BLOCKS, P], "bank_t%d" % u, "A%d" % i)
             for k in range(BLOCKS):
@@ -230,20 +231,20 @@ def tile_list_modp_gelu_resb_kernel(
                 total.rearrange("p (i j) -> p i j", i=BLOCKS), bank_s[:], ACT.Identity, bias=b_sb[:, t : t + 1]
             )
 
-        nc.vector.tensor_copy(
+        nc.scalar.copy(
             wu_w[:].bitcast(U16).rearrange("p (t m) -> p t m", t=PACK),
             wu_w_raw[:].bitcast(U16).rearrange("p (m t) -> p t m", t=PACK),
         )
-        v_s0 = sb([P, CHUNK], U8, "v_s0")
-        nc.vector.tensor_copy(v_s0[:], tab_s[:].bitcast(U8).indirect(listed(0, CHUNK)))
+        v_s0 = sb([P, FIRST], U8, "v_s0")
+        nc.vector.tensor_copy(v_s0[:], tab_s[:].bitcast(U8).indirect(listed(0, FIRST)))
         v_w0 = sb([P, CHUNK], U32, "v_w0")
         gather_words(0, CHUNK, v_w0[:])
         nc.vector.tensor_copy(
             wu_s[:].rearrange("p (t m) -> p t m", t=PACK),
             wu_s_raw[:].bitcast(U8).rearrange("p (m t) -> p t m", t=PACK),
         )
-        v_s = sb([P, J - CHUNK], U8, "v_s", "wu_s_raw")
-        nc.vector.tensor_copy(v_s[:], tab_s[:].bitcast(U8).indirect(listed(CHUNK, J)))
+        v_s = sb([P, J - FIRST], U8, "v_s", "wu_s_raw")
+        nc.vector.tensor_copy(v_s[:], tab_s[:].bitcast(U8).indirect(listed(FIRST, J)))
         wd_bf = sb([P, WD_HALF, PACK], BF16, "wd_bf0")
         nc.scalar.copy(wd_bf[:, 0:P, :], wd_raw[0][:].rearrange("p j n -> p n j"))
         v_w = sb([P, J - CHUNK], U32, "v_w", "wd_raw0")
@@ -255,25 +256,26 @@ def tile_list_modp_gelu_resb_kernel(
 
         def gather_residual(t, a, z, dst):
             nc.vector.tensor_copy(dst, r_tab[t][:].indirect(listed(a, z)))
-            for i in range(a // HALF, z // HALF):
-                picked[(t, i)] = dst[:, i * HALF - a : (i + 1) * HALF - a]
+            for k in range(a // P, z // P):
+                picked[(t, k)] = dst[:, k * P - a : (k + 1) * P - a]
 
         def later(c):
             rest = slice((c - 1) * CHUNK, c * CHUNK)
-            return hidden(c, v_w[:, rest], v_s[:, rest])
+            a, z = c * CHUNK, (c + 1) * CHUNK
+            return hidden(c, v_w[:, rest], v_s0[:, a:z] if z <= FIRST else v_s[:, a - FIRST : z - FIRST])
 
         def both_tiles(c, bank_tags, total):
             a, z = c * CHUNK, (c + 1) * CHUNK
-            y = sb([P, 2, CHUNK], F32, "y_%d" % c)
+            y = placed([P, 2, CHUNK], F32, "y_%d" % c, (18 + 2 * c) * SUM_BYTES)
             for t in range(2):
                 product(t, a, z, y[:, t, :], bank_tags[t])
                 add_residual(t, a, z, y[:, t, :], total[t])
             for t in range(2):
                 place(t, a, z, total[t])
 
-        gather_residual(2, 0, HALF, sb([P, HALF], F32, "picked2_0")[:])
-        quantise_h(0, hidden(0, v_w0[:], v_s0[:]), sb([P, CHUNK], U8, "h_s0"))
-        gather_residual(2, HALF, J, placed([P, HALF], F32, "picked2_1", 11 * SUM_BYTES)[:])
+        gather_residual(2, 0, J - CHUNK, sb([P, J - CHUNK], F32, "picked2_0")[:])
+        quantise_h(0, hidden(0, v_w0[:], v_s0[:, 0:CHUNK]), sb([P, CHUNK], U8, "h_s0"))
+        gather_residual(2, J - CHUNK, J, placed([P, CHUNK], F32, "picked2_1", 12 * SUM_BYTES)[:])
         gather_residual(3, 0, J, sb([P, J], F32, "picked3")[:])
         quantise_h(1, later(1), sb([P, CHUNK], U8, "h_s1"))
         both_tiles(
@@ -313,5 +315,5 @@ def tile_list_modp_gelu_resb_kernel(
         for t in range(2, TILES):
             total = sb([P, J], F32, "late_total%d" % t)
             for i in range(2):
-                late_half(t, i, picked[(t, i)], total[:, HALF * i : HALF * (i + 1)])
+                late_half(t, i, [picked[(t, BLOCKS * i + k)] for k in range(BLOCKS)], total[:, HALF * i : HALF * (i + 1)])
             place(t, 0, J, total[:])

@@ -26,7 +26,6 @@ BLOCKS = HALF // P
 TILES = N // P
 WD_HALF = N // 2
 SUM_BYTES = 4 * CHUNK
-FIRST = 768
 
 
 def tile_list_modp_gelu_resb_kernel(
@@ -54,8 +53,7 @@ def tile_list_modp_gelu_resb_kernel(
         sm_sb = sb([P, PACK], F32, "sm_sb")
         b_sb = sb([P, TILES], F32, "b_sb")
         wgo_all = sb([P, J], F32, "wgo_all")
-        wd_cols = [slice(0, P), slice(P, 2 * P), slice(2 * P, N)]
-        wd_raw = [sb([P, PACK, s.stop - s.start], F32, "wd_raw%d" % i) for i, s in enumerate(wd_cols)]
+        wd_raw = [sb([P, PACK, WD_HALF], F32, "wd_raw%d" % i) for i in range(2)]
         h_s = {}
         h_w = sb([P, J], U32, "h_w")
         r_tab = [sb([P, T], F32, "r_tab%d" % t) for t in range(TILES)]
@@ -97,8 +95,7 @@ def tile_list_modp_gelu_resb_kernel(
         load_scale_rows(tab_s, tab_scales)
         nc.sync.dma_start(tab_w[:], tab_words[0].rearrange("p t i -> p (t i)").bitcast(I32))
         load_scale_rows(wu_s_raw, wu_scales)
-        nc.sync.dma_start(wd_raw[0][:], wd_rows[:, :, wd_cols[0]])
-        nc.sync.dma_start(wd_raw[1][:], wd_rows[:, :, wd_cols[1]])
+        nc.sync.dma_start(wd_raw[0][:], wd_rows[:, :, 0:WD_HALF])
         load_residual(2)
         load_residual(3)
         with nc.allow_non_contiguous_dma(reason="one bias value a partition"):
@@ -108,7 +105,7 @@ def tile_list_modp_gelu_resb_kernel(
         nc.sync.dma_start(wgo_all[:, 0:CHUNK], wgo[:, 0:CHUNK])
         nc.sync.dma_start(wgo_all[:, CHUNK:HALF], wgo[:, CHUNK:HALF])
         nc.sync.dma_start(wgo_all[:, HALF:J], wgo[:, HALF:J])
-        nc.sync.dma_start(wd_raw[2][:], wd_rows[:, :, wd_cols[2]])
+        nc.sync.dma_start(wd_raw[1][:], wd_rows[:, :, WD_HALF:N])
 
         def listed(a, z):
             return offsets[:, a // 16 : z // 16]
@@ -235,21 +232,18 @@ def tile_list_modp_gelu_resb_kernel(
             wu_w[:].bitcast(U16).rearrange("p (t m) -> p t m", t=PACK),
             wu_w_raw[:].bitcast(U16).rearrange("p (m t) -> p t m", t=PACK),
         )
-        v_s0 = sb([P, FIRST], U8, "v_s0")
-        nc.vector.tensor_copy(v_s0[:], tab_s[:].bitcast(U8).indirect(listed(0, FIRST)))
+        v_s = sb([P, J], U8, "v_s")
+        nc.vector.tensor_copy(v_s[:], tab_s[:].bitcast(U8).indirect(offsets[:]))
         v_w0 = sb([P, CHUNK], U32, "v_w0")
         gather_words(0, CHUNK, v_w0[:])
         nc.vector.tensor_copy(
             wu_s[:].rearrange("p (t m) -> p t m", t=PACK),
             wu_s_raw[:].bitcast(U8).rearrange("p (m t) -> p t m", t=PACK),
         )
-        v_s = sb([P, J - FIRST], U8, "v_s", "wu_s_raw")
-        nc.vector.tensor_copy(v_s[:], tab_s[:].bitcast(U8).indirect(listed(FIRST, J)))
-        wd_bf = sb([P, WD_HALF, PACK], BF16, "wd_bf0")
-        nc.scalar.copy(wd_bf[:, 0:P, :], wd_raw[0][:].rearrange("p j n -> p n j"))
-        v_w = sb([P, J - CHUNK], U32, "v_w", "wd_raw0")
-        nc.vector.tensor_copy(wd_bf[:, P : 2 * P, :], wd_raw[1][:].rearrange("p j n -> p n j"))
+        v_w = sb([P, J - CHUNK], U32, "v_w", "wu_s_raw")
         gather_words(CHUNK, J, v_w[:])
+        wd_bf = sb([P, WD_HALF, PACK], BF16, "wd_bf0")
+        nc.vector.tensor_copy(wd_bf[:], wd_raw[0][:].rearrange("p j n -> p n j"))
         quantise_wd(0, wd_bf[:].rearrange("p n j -> p (n j)"), sb([P, WD_HALF], U32, "wd_w0")[:])
 
         picked = {}
@@ -262,7 +256,7 @@ def tile_list_modp_gelu_resb_kernel(
         def later(c):
             rest = slice((c - 1) * CHUNK, c * CHUNK)
             a, z = c * CHUNK, (c + 1) * CHUNK
-            return hidden(c, v_w[:, rest], v_s0[:, a:z] if z <= FIRST else v_s[:, a - FIRST : z - FIRST])
+            return hidden(c, v_w[:, rest], v_s[:, a:z])
 
         def both_tiles(c, bank_tags, total):
             a, z = c * CHUNK, (c + 1) * CHUNK
@@ -274,7 +268,7 @@ def tile_list_modp_gelu_resb_kernel(
                 place(t, a, z, total[t])
 
         gather_residual(2, 0, J - CHUNK, sb([P, J - CHUNK], F32, "picked2_0")[:])
-        quantise_h(0, hidden(0, v_w0[:], v_s0[:, 0:CHUNK]), sb([P, CHUNK], U8, "h_s0"))
+        quantise_h(0, hidden(0, v_w0[:], v_s[:, 0:CHUNK]), sb([P, CHUNK], U8, "h_s0"))
         gather_residual(2, J - CHUNK, J, placed([P, CHUNK], F32, "picked2_1", 12 * SUM_BYTES)[:])
         gather_residual(3, 0, J, sb([P, J], F32, "picked3")[:])
         quantise_h(1, later(1), sb([P, CHUNK], U8, "h_s1"))
@@ -302,7 +296,7 @@ def tile_list_modp_gelu_resb_kernel(
         total = sb([P, CHUNK], F32, "total0_3")
         add_residual(0, J - CHUNK, J, y[:], total[:])
         wd_bf1 = placed([P, WD_HALF, PACK], BF16, "wd_bf1", 3 * SUM_BYTES)
-        nc.scalar.copy(wd_bf1[:], wd_raw[2][:].rearrange("p j n -> p n j"))
+        nc.scalar.copy(wd_bf1[:], wd_raw[1][:].rearrange("p j n -> p n j"))
         codes = sb([P, WD_HALF], U32, "wd_w1")
         quantise_wd(1, wd_bf1[:].rearrange("p n j -> p (n j)"), codes[:])
         place(0, J - CHUNK, J, total[:])

@@ -82,8 +82,9 @@ def tile_list_modp_gelu_resb_kernel(
         nc.scalar.activation(ident[:], near[:], ACT.Relu, bias=no_bias[:])
 
         def load_scale_rows(plane, rows):
-            for q in range(QUADS):
-                nc.sync.dma_start(plane[32 * q : 32 * q + 4, :], rows[0, 4 * q : 4 * q + 4, :].bitcast(I32))
+            by_place = rows[0].rearrange("(q r) c -> r q c", r=4)
+            for r in range(4):
+                nc.sync.dma_start(plane[r:P:32, :], by_place[r].bitcast(I32))
 
         def load_residual(t):
             nc.sync.dma_start(r_tab[t][:], rT[P * t : P * (t + 1), :])

@@ -130,8 +130,7 @@ def tile_list_modp_gelu_resb_kernel(
                         start=True,
                         stop=True,
                     )
-                planes = slice(per_bank * i, per_bank * (i + 1))
-                nc.scalar.activation(act[:, planes, :], a_bank[:], ACT.Gelu_apprx_tanh, bias=no_bias[:])
+                nc.scalar.activation(act[i][:], a_bank[:], ACT.Gelu_apprx_tanh, bias=no_bias[:])
 
         def placed(shape, dtype, name, offset):
             return shared.tile(shape, dtype, name=name, offset=offset, align_bytes=64)
@@ -144,8 +143,8 @@ def tile_list_modp_gelu_resb_kernel(
                 in_=woven[:].rearrange("p n t -> p (n t)"),
             )
 
-        def hidden(c, words, scales):
-            act = placed([P, PACK, CHUNK], F32, "act%d" % c, 7 * SUM_BYTES)
+        def smoothed(c, words, scales):
+            act = [placed([P, 2, CHUNK], F32, "act%d_%d" % (c, i), (7 + 2 * i) * SUM_BYTES) for i in range(2)]
             activated(c * CHUNK, words, scales, act, ["A%d" % (2 * (c % 2) + pair) for pair in range(2)])
             if c == CHUNKS - 1:
                 planes = shared.tile([P, PACK, CHUNK], BF16, name="planes_last", offset=2 * SUM_BYTES, align_bytes=64)
@@ -154,7 +153,10 @@ def tile_list_modp_gelu_resb_kernel(
             else:
                 planes = placed([P, PACK, CHUNK], BF16, "planes%d" % c, (16 + 2 * c) * SUM_BYTES)
             for t in range(PACK):
-                nc.scalar.activation(planes[:, t, :], act[:, t, :], ACT.Copy, scale=sm_sb[:, t : t + 1])
+                nc.scalar.activation(planes[:, t, :], act[t // 2][:, t % 2, :], ACT.Copy, scale=sm_sb[:, t : t + 1])
+            return planes
+
+        def weave(c, planes):
             if c == CHUNKS - 1:
                 woven = placed([P, CHUNK, PACK], BF16, "woven_last", 15 * SUM_BYTES)
             else:
@@ -174,6 +176,14 @@ def tile_list_modp_gelu_resb_kernel(
             )
             for e in range(2):
                 wd_w[2 * i + e] = codes[:, P * e : P * (e + 1)].bitcast(FP8X4)
+
+        def quantise_wd_tile(t, rounded, codes):
+            nc.vector.quantize_mx(
+                out=codes[:].bitcast(FP8X4),
+                scales=wd_s[:, P * t : P * (t + 1)],
+                in_=rounded[:, P * (t % 2) : P * (t % 2 + 1), :].rearrange("p n j -> p (n j)"),
+            )
+            wd_w[t] = codes[:].bitcast(FP8X4)
 
         def place(t, a, z, values):
             win = window[t % 2]
@@ -245,7 +255,6 @@ def tile_list_modp_gelu_resb_kernel(
         gather_words(CHUNK, J, v_w[:])
         wd_bf = sb([P, WD_HALF, PACK], BF16, "wd_bf0")
         nc.vector.tensor_copy(wd_bf[:], wd_raw[0][:].rearrange("p j n -> p n j"))
-        quantise_wd(0, wd_bf[:].rearrange("p n j -> p (n j)"), sb([P, WD_HALF], U32, "wd_w0")[:])
 
         picked = {}
 
@@ -257,54 +266,58 @@ def tile_list_modp_gelu_resb_kernel(
         def later(c):
             rest = slice((c - 1) * CHUNK, c * CHUNK)
             a, z = c * CHUNK, (c + 1) * CHUNK
-            return hidden(c, v_w[:, rest], v_s[:, a:z])
+            return smoothed(c, v_w[:, rest], v_s[:, a:z])
 
-        def both_tiles(c, bank_tags, total):
+        def step(c, bank_tags, total, plane):
             a, z = c * CHUNK, (c + 1) * CHUNK
-            y = placed([P, 2, CHUNK], F32, "y_%d" % c, (18 + 2 * c) * SUM_BYTES)
+            planes = later(c + 1)
+            y = [sb([P, CHUNK], F32, "y0_%d" % c), placed([P, CHUNK], F32, "y1_%d" % c, (18 + 2 * c) * SUM_BYTES)]
+            product(0, a, z, y[0][:], bank_tags[0])
+            quantise_h(c + 1, weave(c + 1, planes), plane)
+            product(1, a, z, y[1][:], bank_tags[1])
             for t in range(2):
-                product(t, a, z, y[:, t, :], bank_tags[t])
-                add_residual(t, a, z, y[:, t, :], total[t])
+                add_residual(t, a, z, y[t][:], total[t])
             for t in range(2):
                 place(t, a, z, total[t])
 
-        gather_residual(2, 0, J - CHUNK, sb([P, J - CHUNK], F32, "picked2_0")[:])
-        quantise_h(0, hidden(0, v_w0[:], v_s[:, 0:CHUNK]), sb([P, CHUNK], U8, "h_s0"))
-        gather_residual(2, J - CHUNK, J, placed([P, CHUNK], F32, "picked2_1", 12 * SUM_BYTES)[:])
-        gather_residual(3, 0, J, sb([P, J], F32, "picked3")[:])
-        quantise_h(1, later(1), sb([P, CHUNK], U8, "h_s1"))
-        both_tiles(
+        gather_residual(2, 0, J, sb([P, J], F32, "picked2")[:])
+        quantise_h(0, weave(0, smoothed(0, v_w0[:], v_s[:, 0:CHUNK])), sb([P, CHUNK], U8, "h_s0"))
+        quantise_wd(0, wd_bf[:].rearrange("p n j -> p (n j)"), placed([P, WD_HALF], U32, "wd_w0", 11 * SUM_BYTES)[:])
+        gather_residual(3, 0, J, placed([P, J], F32, "picked3", 24 * SUM_BYTES)[:])
+        step(
             0,
-            ["A2", "A3"],
+            ["Y1", "A3"],
             [sb([P, CHUNK], F32, "total0_0")[:], placed([P, CHUNK], F32, "total1_0", SUM_BYTES // 2)[:]],
+            sb([P, CHUNK], U8, "h_s1"),
         )
-        quantise_h(2, later(2), sb([P, CHUNK], U8, "h_s2", "total0_0"))
-        both_tiles(
+        step(
             1,
-            ["A0", "A1"],
+            ["Y1", "A1"],
             [placed([P, CHUNK], F32, "total0_1", SUM_BYTES)[:], placed([P, CHUNK], F32, "total1_1", 0)[:]],
+            sb([P, CHUNK], U8, "h_s2", "total0_0"),
         )
 
-        woven = later(3)
+        planes = later(3)
         y = sb([P, CHUNK], F32, "y0_2")
-        product(0, HALF, HALF + CHUNK, y[:], "A2")
+        product(0, HALF, HALF + CHUNK, y[:], "Y1")
+        woven = weave(3, planes)
         total = placed([P, CHUNK], F32, "total0_2", 3 * SUM_BYTES // 2)
         add_residual(0, HALF, HALF + CHUNK, y[:], total[:])
         quantise_h(3, woven, placed([P, CHUNK], U8, "h_s3", 0))
         place(0, HALF, HALF + CHUNK, total[:])
         y = sb([P, CHUNK], F32, "y0_3")
         product(0, J - CHUNK, J, y[:], "Y0")
-        total = sb([P, CHUNK], F32, "total0_3")
+        total = placed([P, CHUNK], F32, "total0_3", 22 * SUM_BYTES)
         add_residual(0, J - CHUNK, J, y[:], total[:])
         wd_bf1 = placed([P, WD_HALF, PACK], BF16, "wd_bf1", 3 * SUM_BYTES)
         nc.scalar.copy(wd_bf1[:], wd_raw[1][:].rearrange("p j n -> p n j"))
-        codes = sb([P, WD_HALF], U32, "wd_w1")
-        quantise_wd(1, wd_bf1[:].rearrange("p n j -> p (n j)"), codes[:])
+        quantise_wd_tile(2, wd_bf1, sb([P, P], U32, "wd_w2"))
         place(0, J - CHUNK, J, total[:])
         y = sb([P, HALF], F32, "y1_23")
         product(1, HALF, J, y[:], "A3")
         total = sb([P, HALF], F32, "total1_23", "y0_3")
         add_residual(1, HALF, J, y[:], total[:])
+        quantise_wd_tile(3, wd_bf1, placed([P, P], U32, "wd_w3", 22 * SUM_BYTES))
         place(1, HALF, J, total[:])
 
         for t in range(2, TILES):

@@ -96,8 +96,8 @@ def tile_list_modp_gelu_resb_kernel(
         load_scale_rows(tab_s, tab_scales)
         nc.sync.dma_start(tab_w[:], tab_words[0].rearrange("p t i -> p (t i)").bitcast(I32))
         load_scale_rows(wu_s_raw, wu_scales)
-        nc.sync.dma_start(wd_raw[0][:], wd_rows[:, :, 0:WD_HALF])
         load_residual(2)
+        nc.sync.dma_start(wd_raw[0][:], wd_rows[:, :, 0:WD_HALF])
         load_residual(3)
         with nc.allow_non_contiguous_dma(reason="one bias value a partition"):
             nc.sync.dma_start(b_sb[:], b.rearrange("(t p) -> p t", p=P))
@@ -253,8 +253,6 @@ def tile_list_modp_gelu_resb_kernel(
         )
         v_w = sb([P, J - CHUNK], U32, "v_w", "wu_s_raw")
         gather_words(CHUNK, J, v_w[:])
-        wd_bf = sb([P, WD_HALF, PACK], BF16, "wd_bf0")
-        nc.vector.tensor_copy(wd_bf[:], wd_raw[0][:].rearrange("p j n -> p n j"))
 
         picked = {}
 
@@ -281,6 +279,8 @@ def tile_list_modp_gelu_resb_kernel(
                 place(t, a, z, total[t])
 
         gather_residual(2, 0, J, sb([P, J], F32, "picked2")[:])
+        wd_bf = sb([P, WD_HALF, PACK], BF16, "wd_bf0")
+        nc.vector.tensor_copy(wd_bf[:], wd_raw[0][:].rearrange("p j n -> p n j"))
         quantise_h(0, weave(0, smoothed(0, v_w0[:], v_s[:, 0:CHUNK])), sb([P, CHUNK], U8, "h_s0"))
         quantise_wd(0, wd_bf[:].rearrange("p n j -> p (n j)"), placed([P, WD_HALF], U32, "wd_w0", 11 * SUM_BYTES)[:])
         gather_residual(3, 0, J, placed([P, J], F32, "picked3", 24 * SUM_BYTES)[:])

@@ -26,6 +26,7 @@ BLOCKS = HALF // P
 TILES = N // P
 WD_HALF = N // 2
 SUM_BYTES = 4 * CHUNK
+BANK_BYTES = 2048
 
 
 def tile_list_modp_gelu_resb_kernel(
@@ -40,8 +41,8 @@ def tile_list_modp_gelu_resb_kernel(
         def sb(shape, dtype, name, tag=None):
             return keep.tile(shape, dtype, name=name, tag=tag or name, align_bytes=64)
 
-        def bank(shape, name, tag):
-            return psum.tile(shape, F32, name=name, tag=tag)
+        def bank(shape, name, number):
+            return psum.tile(shape, F32, name=name, offset=number * BANK_BYTES)
 
         offsets = keep.tile([P, J // 16], U16, name="offsets")
         tab_w = sb([P, T], I32, "tab_w")
@@ -145,7 +146,7 @@ def tile_list_modp_gelu_resb_kernel(
 
         def smoothed(c, words, scales):
             act = [placed([P, 2, CHUNK], F32, "act%d_%d" % (c, i), (7 + 2 * i) * SUM_BYTES) for i in range(2)]
-            activated(c * CHUNK, words, scales, act, ["A%d" % (2 * (c % 2) + pair) for pair in range(2)])
+            activated(c * CHUNK, words, scales, act, [2 * (c % 2) + pair for pair in range(2)])
             if c == CHUNKS - 1:
                 planes = shared.tile([P, PACK, CHUNK], BF16, name="planes_last", offset=2 * SUM_BYTES, align_bytes=64)
             elif c == 0:
@@ -211,12 +212,12 @@ def tile_list_modp_gelu_resb_kernel(
         def late_half(t, i, picked, total):
             u = 2 * t + i
             a = i * HALF
-            bank_r = bank([P, BLOCKS, P], "bank_r%d" % u, "Y0" if i == 0 else "A3")
+            bank_r = bank([P, BLOCKS, P], "bank_r%d" % u, [4, 7][i] if t == 2 else 6)
             for k in range(BLOCKS):
                 nc.tensor.transpose(bank_r[:, k, :], picked[k], ident[:])
-            r_turned = placed([P, BLOCKS, P], F32, "r_turned%d" % u, (14 + 2 * i) * SUM_BYTES)
+            r_turned = placed([P, BLOCKS, P], F32, "r_turned%d" % u, (14 + 2 * ((t + i) % 2)) * SUM_BYTES)
             nc.scalar.copy(r_turned[:], bank_r[:])
-            bank_t = bank([P, BLOCKS, P], "bank_t%d" % u, "A%d" % i)
+            bank_t = bank([P, BLOCKS, P], "bank_t%d" % u, i if t == 2 else 2)
             for k in range(BLOCKS):
                 nc.tensor.matmul_mx(
                     out=bank_t[:, k, :],
@@ -229,7 +230,7 @@ def tile_list_modp_gelu_resb_kernel(
                 )
             y_turned = sb([P, BLOCKS, P], F32, "y_turned%d" % u)
             nc.scalar.copy(y_turned[:], bank_t[:])
-            bank_s = bank([P, BLOCKS, P], "bank_s%d" % u, "S%d" % i)
+            bank_s = bank([P, BLOCKS, P], "bank_s%d" % u, [6, 2][i] if t == 2 else i)
             for k in range(BLOCKS):
                 nc.tensor.matmul(bank_s[:, k, :], r_turned[:, k, :], ident[:], start=k == 0, stop=False, is_transpose=True)
             for k in range(BLOCKS):
@@ -286,27 +287,27 @@ def tile_list_modp_gelu_resb_kernel(
         gather_residual(3, 0, J, placed([P, J], F32, "picked3", 24 * SUM_BYTES)[:])
         step(
             0,
-            ["Y1", "A3"],
+            [5, 3],
             [sb([P, CHUNK], F32, "total0_0")[:], placed([P, CHUNK], F32, "total1_0", SUM_BYTES // 2)[:]],
             sb([P, CHUNK], U8, "h_s1"),
         )
         step(
             1,
-            ["Y1", "A1"],
+            [5, 1],
             [placed([P, CHUNK], F32, "total0_1", SUM_BYTES)[:], placed([P, CHUNK], F32, "total1_1", 0)[:]],
             sb([P, CHUNK], U8, "h_s2", "total0_0"),
         )
 
         planes = later(3)
         y = sb([P, CHUNK], F32, "y0_2")
-        product(0, HALF, HALF + CHUNK, y[:], "Y1")
+        product(0, HALF, HALF + CHUNK, y[:], 5)
         woven = weave(3, planes)
         total = placed([P, CHUNK], F32, "total0_2", 3 * SUM_BYTES // 2)
         add_residual(0, HALF, HALF + CHUNK, y[:], total[:])
         quantise_h(3, woven, placed([P, CHUNK], U8, "h_s3", 0))
         place(0, HALF, HALF + CHUNK, total[:])
         y = sb([P, CHUNK], F32, "y0_3")
-        product(0, J - CHUNK, J, y[:], "Y0")
+        product(0, J - CHUNK, J, y[:], 5)
         total = placed([P, CHUNK], F32, "total0_3", 22 * SUM_BYTES)
         add_residual(0, J - CHUNK, J, y[:], total[:])
         wd_bf1 = placed([P, WD_HALF, PACK], BF16, "wd_bf1", 3 * SUM_BYTES)
@@ -314,7 +315,7 @@ def tile_list_modp_gelu_resb_kernel(
         quantise_wd_tile(2, wd_bf1, sb([P, P], U32, "wd_w2"))
         place(0, J - CHUNK, J, total[:])
         y = sb([P, HALF], F32, "y1_23")
-        product(1, HALF, J, y[:], "A3")
+        product(1, HALF, J, y[:], 3)
         total = sb([P, HALF], F32, "total1_23", "y0_3")
         add_residual(1, HALF, J, y[:], total[:])
         quantise_wd_tile(3, wd_bf1, placed([P, P], U32, "wd_w3", 22 * SUM_BYTES))

@@ -48,7 +48,7 @@ def tile_list_modp_gelu_resb_kernel(
         tab_w = sb([P, T], I32, "tab_w")
         tab_s = sb([P, T // 4], I32, "tab_s")
         wu_w_raw = sb([P, R // 2], I32, "wu_w_raw")
-        wu_s_raw = sb([P, R // 4], I32, "wu_s_raw")
+        wu_s_raw = shared.tile([P, R // 4], I32, name="wu_s_raw", offset=32 * SUM_BYTES, align_bytes=64)
         wu_w = sb([P, 2 * R], U8, "wu_w")
         wu_s = sb([P, R], U8, "wu_s")
         sm_sb = sb([P, PACK], F32, "sm_sb")
@@ -144,15 +144,18 @@ def tile_list_modp_gelu_resb_kernel(
                 in_=woven[:].rearrange("p n t -> p (n t)"),
             )
 
+        act_at = [(7, 9), (7, 9), (9, 19), (19, 29)]
+        planes_at = {1: 18, 2: 28}
+
         def smoothed(c, words, scales):
-            act = [placed([P, 2, CHUNK], F32, "act%d_%d" % (c, i), (7 + 2 * i) * SUM_BYTES) for i in range(2)]
+            act = [placed([P, 2, CHUNK], F32, "act%d_%d" % (c, i), act_at[c][i] * SUM_BYTES) for i in range(2)]
             activated(c * CHUNK, words, scales, act, [2 * (c % 2) + pair for pair in range(2)])
             if c == CHUNKS - 1:
                 planes = shared.tile([P, PACK, CHUNK], BF16, name="planes_last", offset=2 * SUM_BYTES, align_bytes=64)
             elif c == 0:
                 planes = placed([P, PACK, CHUNK], BF16, "planes0", 11 * SUM_BYTES)
             else:
-                planes = placed([P, PACK, CHUNK], BF16, "planes%d" % c, (16 + 2 * c) * SUM_BYTES)
+                planes = placed([P, PACK, CHUNK], BF16, "planes%d" % c, planes_at[c] * SUM_BYTES)
             for t in range(PACK):
                 nc.scalar.activation(planes[:, t, :], act[t // 2][:, t % 2, :], ACT.Copy, scale=sm_sb[:, t : t + 1])
             return planes
@@ -244,16 +247,18 @@ def tile_list_modp_gelu_resb_kernel(
             wu_w[:].bitcast(U16).rearrange("p (t m) -> p t m", t=PACK),
             wu_w_raw[:].bitcast(U16).rearrange("p (m t) -> p t m", t=PACK),
         )
-        v_s = sb([P, J], U8, "v_s")
-        nc.vector.tensor_copy(v_s[:], tab_s[:].bitcast(U8).indirect(offsets[:]))
+        v_s = sb([P, J - CHUNK], U8, "v_s")
+        nc.vector.tensor_copy(v_s[:], tab_s[:].bitcast(U8).indirect(listed(0, J - CHUNK)))
         v_w0 = sb([P, CHUNK], U32, "v_w0")
         gather_words(0, CHUNK, v_w0[:])
         nc.vector.tensor_copy(
             wu_s[:].rearrange("p (t m) -> p t m", t=PACK),
             wu_s_raw[:].bitcast(U8).rearrange("p (m t) -> p t m", t=PACK),
         )
-        v_w = sb([P, J - CHUNK], U32, "v_w", "wu_s_raw")
+        v_w = placed([P, J - CHUNK], U32, "v_w", 32 * SUM_BYTES + CHUNK)
         gather_words(CHUNK, J, v_w[:])
+        v_s_last = placed([P, CHUNK], U8, "v_s_last", 32 * SUM_BYTES)
+        nc.vector.tensor_copy(v_s_last[:], tab_s[:].bitcast(U8).indirect(listed(J - CHUNK, J)))
 
         picked = {}
 
@@ -265,14 +270,15 @@ def tile_list_modp_gelu_resb_kernel(
         def later(c):
             rest = slice((c - 1) * CHUNK, c * CHUNK)
             a, z = c * CHUNK, (c + 1) * CHUNK
-            return smoothed(c, v_w[:, rest], v_s[:, a:z])
+            return smoothed(c, v_w[:, rest], v_s_last[:] if z == J else v_s[:, a:z])
 
         def step(c, bank_tags, total, plane):
             a, z = c * CHUNK, (c + 1) * CHUNK
             planes = later(c + 1)
-            y = [sb([P, CHUNK], F32, "y0_%d" % c), placed([P, CHUNK], F32, "y1_%d" % c, (18 + 2 * c) * SUM_BYTES)]
+            y = [placed([P, CHUNK], F32, "y0_%d" % c, act_at[c + 1][0] * SUM_BYTES)]
             product(0, a, z, y[0][:], bank_tags[0])
             quantise_h(c + 1, weave(c + 1, planes), plane)
+            y.append(placed([P, CHUNK], F32, "y1_%d" % c, planes_at[c + 1] * SUM_BYTES))
             product(1, a, z, y[1][:], bank_tags[1])
             for t in range(2):
                 add_residual(t, a, z, y[t][:], total[t])
@@ -299,7 +305,7 @@ def tile_list_modp_gelu_resb_kernel(
         )
 
         planes = later(3)
-        y = sb([P, CHUNK], F32, "y0_2")
+        y = placed([P, CHUNK], F32, "y0_2", act_at[3][0] * SUM_BYTES)
         product(0, HALF, HALF + CHUNK, y[:], 5)
         woven = weave(3, planes)
         total = placed([P, CHUNK], F32, "total0_2", 3 * SUM_BYTES // 2)

@@ -181,11 +181,16 @@ def tile_list_modp_gelu_resb_kernel(
             for e in range(2):
                 wd_w[2 * i + e] = codes[:, P * e : P * (e + 1)].bitcast(FP8X4)
 
+        def rounded_wd(t, offset):
+            rounded = placed([P, P, PACK], BF16, "wd_bf%d" % t, offset)
+            nc.scalar.copy(rounded[:], wd_raw[1][:, :, P * (t % 2) : P * (t % 2 + 1)].rearrange("p j n -> p n j"))
+            return rounded
+
         def quantise_wd_tile(t, rounded, codes):
             nc.vector.quantize_mx(
                 out=codes[:].bitcast(FP8X4),
                 scales=wd_s[:, P * t : P * (t + 1)],
-                in_=rounded[:, P * (t % 2) : P * (t % 2 + 1), :].rearrange("p n j -> p (n j)"),
+                in_=rounded[:].rearrange("p n j -> p (n j)"),
             )
             wd_w[t] = codes[:].bitcast(FP8X4)
 
@@ -215,12 +220,12 @@ def tile_list_modp_gelu_resb_kernel(
         def late_half(t, i, picked, total):
             u = 2 * t + i
             a = i * HALF
-            bank_r = bank([P, BLOCKS, P], "bank_r%d" % u, [4, 7][i] if t == 2 else 6)
+            bank_r = bank([P, BLOCKS, P], "bank_r%d" % u, [4, 7][i])
             for k in range(BLOCKS):
                 nc.tensor.transpose(bank_r[:, k, :], picked[k], ident[:])
-            r_turned = placed([P, BLOCKS, P], F32, "r_turned%d" % u, (14 + 2 * ((t + i) % 2)) * SUM_BYTES)
+            r_turned = placed([P, BLOCKS, P], F32, "r_turned%d" % u, ([14, 16][i] if t == 2 else [17, 15][i]) * SUM_BYTES)
             nc.scalar.copy(r_turned[:], bank_r[:])
-            bank_t = bank([P, BLOCKS, P], "bank_t%d" % u, i if t == 2 else 2)
+            bank_t = bank([P, BLOCKS, P], "bank_t%d" % u, i if t == 2 else [6, 2][i])
             for k in range(BLOCKS):
                 nc.tensor.matmul_mx(
                     out=bank_t[:, k, :],
@@ -316,15 +321,13 @@ def tile_list_modp_gelu_resb_kernel(
         product(0, J - CHUNK, J, y[:], 5)
         total = placed([P, CHUNK], F32, "total0_3", 22 * SUM_BYTES)
         add_residual(0, J - CHUNK, J, y[:], total[:])
-        wd_bf1 = placed([P, WD_HALF, PACK], BF16, "wd_bf1", 3 * SUM_BYTES)
-        nc.scalar.copy(wd_bf1[:], wd_raw[1][:].rearrange("p j n -> p n j"))
-        quantise_wd_tile(2, wd_bf1, sb([P, P], U32, "wd_w2"))
+        quantise_wd_tile(2, rounded_wd(2, 3 * SUM_BYTES), sb([P, P], U32, "wd_w2"))
         place(0, J - CHUNK, J, total[:])
         y = sb([P, HALF], F32, "y1_23")
         product(1, HALF, J, y[:], 3)
         total = sb([P, HALF], F32, "total1_23", "y0_3")
         add_residual(1, HALF, J, y[:], total[:])
-        quantise_wd_tile(3, wd_bf1, placed([P, P], U32, "wd_w3", 22 * SUM_BYTES))
+        quantise_wd_tile(3, rounded_wd(3, 19 * SUM_BYTES), placed([P, P], U32, "wd_w3", 22 * SUM_BYTES))
         place(1, HALF, J, total[:])
 
         for t in range(2, TILES):

@@ -50,7 +50,7 @@ def tile_list_modp_gelu_resb_kernel(
         wu_w_raw = sb([P, R // 2], I32, "wu_w_raw")
         wu_s_raw = shared.tile([P, R // 4], I32, name="wu_s_raw", offset=32 * SUM_BYTES, align_bytes=64)
         wu_w = sb([P, 2 * R], U8, "wu_w")
-        wu_s = sb([P, R], U8, "wu_s")
+        wu_s = [sb([P, 2, P], U8, "wu_s%d" % pair) for pair in range(2)]
         sm_sb = sb([P, PACK], F32, "sm_sb")
         b_sb = sb([P, TILES], F32, "b_sb")
         wgo_all = sb([P, J], F32, "wgo_all")
@@ -58,7 +58,7 @@ def tile_list_modp_gelu_resb_kernel(
         h_s = {}
         h_w = sb([P, J], U32, "h_w")
         r_tab = [sb([P, T], F32, "r_tab%d" % t) for t in range(TILES)]
-        window = [sb([P, T], F32, "window%d" % i) for i in range(2)]
+        window = [sb([P, T], F32, "window0")]
         zero = sb([P, 1], F32, "zero")
         ident = sb([P, P], F32, "ident")
 
@@ -70,7 +70,6 @@ def tile_list_modp_gelu_resb_kernel(
         nc.vector.memset(zero[:], 0.0)
         nc.vector.memset(wu_s_raw[:], 0)
         nc.vector.memset(window[0][:].bitcast(I32), 0)
-        nc.vector.memset(window[1][:].bitcast(I32), 0)
         no_bias = sb([P, 1], F32, "no_bias")
         nc.scalar.activation(no_bias[:], zero[:], ACT.Gelu_apprx_tanh)
         for step in range(7):
@@ -117,21 +116,21 @@ def tile_list_modp_gelu_resb_kernel(
 
         def activated(a, words, scales, act, tags):
             width = words.shape[1]
-            per_bank = PACK // len(tags)
-            for i, tag in enumerate(tags):
-                a_bank = bank([P, per_bank, width], "a%d_%d" % (a, i), tag)
-                for u in range(per_bank):
-                    t = per_bank * i + u
+            for first, count, number in tags:
+                a_bank = bank([P, count, width], "a%d_%d" % (a, first), number)
+                for u in range(count):
+                    t = first + u
                     nc.tensor.matmul_mx(
                         out=a_bank[:, u, :],
                         lhsT=wu_w[:, 2 * P * t : 2 * P * (t + 1)].bitcast(FP4X4),
-                        lhsT_scale=wu_s[:, P * t : P * (t + 1)],
+                        lhsT_scale=wu_s[t // 2][:, t % 2, :],
                         rhs=words.bitcast(FP8X4),
                         rhs_scale=scales,
                         start=True,
                         stop=True,
                     )
-                nc.scalar.activation(act[i][:], a_bank[:], ACT.Gelu_apprx_tanh, bias=no_bias[:])
+                slots = slice(first % 2, first % 2 + count)
+                nc.scalar.activation(act[first // 2][:, slots, :], a_bank[:], ACT.Gelu_apprx_tanh, bias=no_bias[:])
 
         def placed(shape, dtype, name, offset):
             return shared.tile(shape, dtype, name=name, offset=offset, align_bytes=64)
@@ -149,7 +148,10 @@ def tile_list_modp_gelu_resb_kernel(
 
         def smoothed(c, words, scales):
             act = [placed([P, 2, CHUNK], F32, "act%d_%d" % (c, i), act_at[c][i] * SUM_BYTES) for i in range(2)]
-            activated(c * CHUNK, words, scales, act, [2 * (c % 2) + pair for pair in range(2)])
+            groups = [(2 * pair, 2, 2 * (c % 2) + pair) for pair in range(2)]
+            if c == 0:
+                groups = [(0, 1, 4), (1, 1, 0), (2, 2, 1)]
+            activated(c * CHUNK, words, scales, act, groups)
             if c == CHUNKS - 1:
                 planes = shared.tile([P, PACK, CHUNK], BF16, name="planes_last", offset=2 * SUM_BYTES, align_bytes=64)
             elif c == 0:
@@ -163,6 +165,8 @@ def tile_list_modp_gelu_resb_kernel(
         def weave(c, planes):
             if c == CHUNKS - 1:
                 woven = placed([P, CHUNK, PACK], BF16, "woven_last", 15 * SUM_BYTES)
+            elif c == 1:
+                woven = placed([P, CHUNK, PACK], BF16, "woven1", 43 * SUM_BYTES)
             else:
                 woven = sb([P, CHUNK, PACK], BF16, "woven%d" % c)
             nc.scalar.copy(
@@ -252,18 +256,15 @@ def tile_list_modp_gelu_resb_kernel(
             wu_w[:].bitcast(U16).rearrange("p (t m) -> p t m", t=PACK),
             wu_w_raw[:].bitcast(U16).rearrange("p (m t) -> p t m", t=PACK),
         )
-        v_s = sb([P, J - CHUNK], U8, "v_s")
-        nc.vector.tensor_copy(v_s[:], tab_s[:].bitcast(U8).indirect(listed(0, J - CHUNK)))
+        v_s = sb([P, J], U8, "v_s")
+        nc.vector.tensor_copy(v_s[:], tab_s[:].bitcast(U8).indirect(offsets[:]))
         v_w0 = sb([P, CHUNK], U32, "v_w0")
         gather_words(0, CHUNK, v_w0[:])
-        nc.vector.tensor_copy(
-            wu_s[:].rearrange("p (t m) -> p t m", t=PACK),
-            wu_s_raw[:].bitcast(U8).rearrange("p (m t) -> p t m", t=PACK),
-        )
+        by_slot = wu_s_raw[:].bitcast(U8).rearrange("p (m t) -> p t m", t=PACK)
+        nc.vector.tensor_copy(wu_s[0][:], by_slot[:, 0:2, :])
+        nc.vector.tensor_copy(wu_s[1][:], by_slot[:, 2:4, :])
         v_w = placed([P, J - CHUNK], U32, "v_w", 32 * SUM_BYTES + CHUNK)
         gather_words(CHUNK, J, v_w[:])
-        v_s_last = placed([P, CHUNK], U8, "v_s_last", 32 * SUM_BYTES)
-        nc.vector.tensor_copy(v_s_last[:], tab_s[:].bitcast(U8).indirect(listed(J - CHUNK, J)))
 
         picked = {}
 
@@ -275,7 +276,7 @@ def tile_list_modp_gelu_resb_kernel(
         def later(c):
             rest = slice((c - 1) * CHUNK, c * CHUNK)
             a, z = c * CHUNK, (c + 1) * CHUNK
-            return smoothed(c, v_w[:, rest], v_s_last[:] if z == J else v_s[:, a:z])
+            return smoothed(c, v_w[:, rest], v_s[:, a:z])
 
         def step(c, bank_tags, total, plane):
             a, z = c * CHUNK, (c + 1) * CHUNK
@@ -283,6 +284,9 @@ def tile_list_modp_gelu_resb_kernel(
             y = [placed([P, CHUNK], F32, "y0_%d" % c, act_at[c + 1][0] * SUM_BYTES)]
             product(0, a, z, y[0][:], bank_tags[0])
             quantise_h(c + 1, weave(c + 1, planes), plane)
+            if c == 0:
+                window.append(placed([P, T], F32, "window1", 36 * SUM_BYTES))
+                nc.gpsimd.memset(window[1][:].bitcast(I32), 0)
             y.append(placed([P, CHUNK], F32, "y1_%d" % c, planes_at[c + 1] * SUM_BYTES))
             product(1, a, z, y[1][:], bank_tags[1])
             for t in range(2):

from contextlib import ExitStack

import concourse.mybir as mybir

K, R, N, T, J = 512, 512, 512, 2048, 1024
FLOPS = 2 * K * R * J + 2 * R * N * J

F32 = mybir.dt.float32
BF16 = mybir.dt.bfloat16
I32 = mybir.dt.int32
U32 = mybir.dt.uint32
U16 = mybir.dt.uint16
U8 = mybir.dt.uint8
FP8X4 = mybir.dt.float8_e4m3fn_x4
FP4X4 = mybir.dt.float4_e2m1fn_x4
ACT = mybir.ActivationFunctionType
ALU = mybir.AluOpType

P = 128
PACK = 4
QUADS = 4
CHUNK = 256
CHUNKS = J // CHUNK
HALF = J // 2
BLOCKS = HALF // P
TILES = N // P
WD_HALF = N // 2
SUM_BYTES = 4 * CHUNK
BANK_BYTES = 2048


def tile_list_modp_gelu_resb_kernel(
    tc, tab_words, tab_scales, wu_words, wu_scales, sm, wd, rT, b, wgo, offs, out
):
    nc = tc.nc
    with ExitStack() as ctx:
        keep = ctx.enter_context(tc.tile_pool(name="keep", bufs=1))
        shared = ctx.enter_context(tc.tile_pool(name="shared", bufs=1))
        psum = ctx.enter_context(tc.psum_pool(name="psum", bufs=1))

        def sb(shape, dtype, name, tag=None):
            return keep.tile(shape, dtype, name=name, tag=tag or name, align_bytes=64)

        def bank(shape, name, number):
            return psum.tile(shape, F32, name=name, offset=number * BANK_BYTES)

        offsets = keep.tile([P, J // 16], U16, name="offsets")
        tab_w = sb([P, T], I32, "tab_w")
        tab_s = sb([P, T // 4], I32, "tab_s")
        wu_w_raw = sb([P, R // 2], I32, "wu_w_raw")
        wu_s_raw = shared.tile([P, R // 4], I32, name="wu_s_raw", offset=32 * SUM_BYTES, align_bytes=64)
        wu_w = sb([P, 2 * R], U8, "wu_w")
        wu_s = [sb([P, 2, P], U8, "wu_s%d" % pair) for pair in range(2)]
        sm_sb = sb([P, PACK], F32, "sm_sb")
        b_sb = sb([P, TILES], F32, "b_sb")
        wgo_all = sb([P, J], F32, "wgo_all")
        wd_raw = [sb([P, PACK, WD_HALF], F32, "wd_raw%d" % i) for i in range(2)]
        h_s = {}
        h_w = sb([P, J], U32, "h_w")
        r_tab = [sb([P, T], F32, "r_tab%d" % t) for t in range(TILES)]
        window = [sb([P, T], F32, "window0")]
        zero = sb([P, 1], F32, "zero")
        ident = sb([P, P], F32, "ident")

        nc.vector.memset(tab_s[:], 0)
        distance = sb([P, P], F32, "distance")
        nc.gpsimd.iota(
            distance[:, 0:1], [[0, 1]], base=0, channel_multiplier=-1, allow_small_or_imprecise_dtypes=True
        )
        nc.vector.memset(zero[:], 0.0)
        nc.vector.memset(wu_s_raw[:], 0)
        nc.vector.memset(window[0][:].bitcast(I32), 0)
        no_bias = sb([P, 1], F32, "no_bias")
        nc.scalar.activation(no_bias[:], zero[:], ACT.Gelu_apprx_tanh)
        for step in range(7):
            width = 2**step
            nc.scalar.activation(distance[:, width : 2 * width], distance[:, 0:width], ACT.Copy, bias=float(width))
        apart = sb([P, P], F32, "apart")
        nc.scalar.activation(apart[:], distance[:], ACT.Abs, bias=no_bias[:])
        near = sb([P, P], F32, "near")
        nc.scalar.activation(near[:], apart[:], ACT.Copy, bias=1.0, scale=-1.0)
        nc.scalar.activation(ident[:], near[:], ACT.Relu, bias=no_bias[:])

        def load_scale_rows(plane, rows):
            by_place = rows[0].rearrange("(q r) c -> r q c", r=4)
            for r in range(4):
                nc.sync.dma_start(plane[r:P:32, :], by_place[r].bitcast(I32))

        def load_residual(t):
            nc.sync.dma_start(r_tab[t][:], rT[P * t : P * (t + 1), :])

        wd_rows = wd.rearrange("(p j) n -> p j n", j=PACK)
        nc.sync.dma_start(offsets[:], offs)
        nc.sync.dma_start(sm_sb[:], sm.rearrange("(p t) -> p t", t=PACK))
        nc.sync.dma_start(wu_w_raw[:], wu_words[0].bitcast(I32))
        load_scale_rows(tab_s, tab_scales)
        nc.sync.dma_start(tab_w[:], tab_words[0].rearrange("p t i -> p (t i)").bitcast(I32))
        load_scale_rows(wu_s_raw, wu_scales)
        load_residual(2)
        nc.sync.dma_start(wd_raw[0][:], wd_rows[:, :, 0:WD_HALF])
        load_residual(3)
        with nc.allow_non_contiguous_dma(reason="one bias value a partition"):
            nc.sync.dma_start(b_sb[:], b.rearrange("(t p) -> p t", p=P))
        load_residual(0)
        load_residual(1)
        nc.sync.dma_start(wgo_all[:, 0:CHUNK], wgo[:, 0:CHUNK])
        nc.sync.dma_start(wgo_all[:, CHUNK:HALF], wgo[:, CHUNK:HALF])
        nc.sync.dma_start(wgo_all[:, HALF:J], wgo[:, HALF:J])
        nc.sync.dma_start(wd_raw[1][:], wd_rows[:, :, WD_HALF:N])

        def listed(a, z):
            return offsets[:, a // 16 : z // 16]

        def gather_words(a, z, dst):
            nc.vector.tensor_copy(dst, tab_w[:].bitcast(U32).indirect(listed(a, z)))

        def activated(a, words, scales, act, tags):
            width = words.shape[1]
            for first, count, number in tags:
                a_bank = bank([P, count, width], "a%d_%d" % (a, first), number)
                for u in range(count):
                    t = first + u
                    nc.tensor.matmul_mx(
                        out=a_bank[:, u, :],
                        lhsT=wu_w[:, 2 * P * t : 2 * P * (t + 1)].bitcast(FP4X4),
                        lhsT_scale=wu_s[t // 2][:, t % 2, :],
                        rhs=words.bitcast(FP8X4),
                        rhs_scale=scales,
                        start=True,
                        stop=True,
                    )
                slots = slice(first % 2, first % 2 + count)
                nc.scalar.activation(act[first // 2][:, slots, :], a_bank[:], ACT.Gelu_apprx_tanh, bias=no_bias[:])

        def placed(shape, dtype, name, offset):
            return shared.tile(shape, dtype, name=name, offset=offset, align_bytes=64)

        def quantise_h(c, woven, plane):
            h_s[c] = plane
            nc.vector.quantize_mx(
                out=h_w[:, c * CHUNK : (c + 1) * CHUNK].bitcast(FP8X4),
                scales=h_s[c][:],
                in_=woven[:].rearrange("p n t -> p (n t)"),
            )

        act_at = [(7, 9), (7, 9), (9, 19), (19, 29)]
        planes_at = {1: 18, 2: 28}

        def smoothed(c, words, scales):
            act = [placed([P, 2, CHUNK], F32, "act%d_%d" % (c, i), act_at[c][i] * SUM_BYTES) for i in range(2)]
            groups = [(2 * pair, 2, 2 * (c % 2) + pair) for pair in range(2)]
            if c == 0:
                groups = [(0, 1, 4), (1, 1, 0), (2, 2, 1)]
            activated(c * CHUNK, words, scales, act, groups)
            if c == CHUNKS - 1:
                planes = shared.tile([P, PACK, CHUNK], BF16, name="planes_last", offset=2 * SUM_BYTES, align_bytes=64)
            elif c == 0:
                planes = placed([P, PACK, CHUNK], BF16, "planes0", 11 * SUM_BYTES)
            else:
                planes = placed([P, PACK, CHUNK], BF16, "planes%d" % c, planes_at[c] * SUM_BYTES)
            for t in range(PACK):
                nc.scalar.activation(planes[:, t, :], act[t // 2][:, t % 2, :], ACT.Copy, scale=sm_sb[:, t : t + 1])
            return planes

        def weave(c, planes):
            if c == CHUNKS - 1:
                woven = placed([P, CHUNK, PACK], BF16, "woven_last", 15 * SUM_BYTES)
            elif c == 1:
                woven = placed([P, CHUNK, PACK], BF16, "woven1", 43 * SUM_BYTES)
            else:
                woven = sb([P, CHUNK, PACK], BF16, "woven%d" % c)
            nc.scalar.copy(
                woven[:].rearrange("p (c i) t -> p c t i", i=4),
                planes[:].rearrange("p t (c i) -> p c t i", i=4),
            )
            return woven

        wd_w = {}
        wd_s = sb([P, N], U8, "wd_s")

        def quantise_wd(i, flat, codes):
            nc.vector.quantize_mx(
                out=codes.bitcast(FP8X4), scales=wd_s[:, WD_HALF * i : WD_HALF * (i + 1)], in_=flat
            )
            for e in range(2):
                wd_w[2 * i + e] = codes[:, P * e : P * (e + 1)].bitcast(FP8X4)

        def rounded_wd(t, offset):
            rounded = placed([P, P, PACK], BF16, "wd_bf%d" % t, offset)
            nc.scalar.copy(rounded[:], wd_raw[1][:, :, P * (t % 2) : P * (t % 2 + 1)].rearrange("p j n -> p n j"))
            return rounded

        def quantise_wd_tile(t, rounded, codes):
            nc.vector.quantize_mx(
                out=codes[:].bitcast(FP8X4),
                scales=wd_s[:, P * t : P * (t + 1)],
                in_=rounded[:].rearrange("p n j -> p (n j)"),
            )
            wd_w[t] = codes[:].bitcast(FP8X4)

        def place(t, a, z, values):
            win = window[t % 2]
            nc.vector.tensor_tensor(win[:].indirect(listed(a, z)), values, wgo_all[:, a:z], ALU.mult)
            if z == J:
                nc.sync.dma_start(out[P * t : P * (t + 1), :], win[:])

        def product(t, a, z, y, tag):
            y_bank = bank([P, z - a], "y%d_%d" % (t, a), tag)
            for c in range(a // CHUNK, z // CHUNK):
                nc.tensor.matmul_mx(
                    out=y_bank[:, c * CHUNK - a : (c + 1) * CHUNK - a],
                    lhsT=wd_w[t],
                    lhsT_scale=wd_s[:, P * t : P * (t + 1)],
                    rhs=h_w[:, c * CHUNK : (c + 1) * CHUNK].bitcast(FP8X4),
                    rhs_scale=h_s[c][:],
                    start=True,
                    stop=True,
                )
            nc.scalar.activation(y, y_bank[:], ACT.Identity, bias=b_sb[:, t : t + 1])

        def add_residual(t, a, z, y, total):
            nc.vector.tensor_tensor(total, r_tab[t][:].indirect(listed(a, z)), y, ALU.add)

        def late_half(t, i, picked, total):
            u = 2 * t + i
            a = i * HALF
            bank_r = bank([P, BLOCKS, P], "bank_r%d" % u, [4, 7][i])
            for k in range(BLOCKS):
                nc.tensor.transpose(bank_r[:, k, :], picked[k], ident[:])
            r_turned = placed([P, BLOCKS, P], F32, "r_turned%d" % u, ([14, 16][i] if t == 2 else [17, 15][i]) * SUM_BYTES)
            nc.scalar.copy(r_turned[:], bank_r[:])
            bank_t = bank([P, BLOCKS, P], "bank_t%d" % u, i if t == 2 else [6, 2][i])
            for k in range(BLOCKS):
                nc.tensor.matmul_mx(
                    out=bank_t[:, k, :],
                    lhsT=h_w[:, a + P * k : a + P * (k + 1)].bitcast(FP8X4),
                    lhsT_scale=h_s[2 * i + k // 2][:, P * (k % 2) : P * (k % 2 + 1)],
                    rhs=wd_w[t],
                    rhs_scale=wd_s[:, P * t : P * (t + 1)],
                    start=True,
                    stop=True,
                )
            y_turned = sb([P, BLOCKS, P], F32, "y_turned%d" % u)
            nc.scalar.copy(y_turned[:], bank_t[:])
            bank_s = bank([P, BLOCKS, P], "bank_s%d" % u, [6, 2][i] if t == 2 else i)
            for k in range(BLOCKS):
                nc.tensor.matmul(bank_s[:, k, :], r_turned[:, k, :], ident[:], start=k == 0, stop=False, is_transpose=True)
            for k in range(BLOCKS):
                last = k == BLOCKS - 1
                nc.tensor.matmul(bank_s[:, k, :], y_turned[:, k, :], ident[:], start=False, stop=last, is_transpose=True)
            nc.scalar.activation(
                total.rearrange("p (i j) -> p i j", i=BLOCKS), bank_s[:], ACT.Identity, bias=b_sb[:, t : t + 1]
            )

        nc.scalar.copy(
            wu_w[:].bitcast(U16).rearrange("p (t m) -> p t m", t=PACK),
            wu_w_raw[:].bitcast(U16).rearrange("p (m t) -> p t m", t=PACK),
        )
        v_s = sb([P, J], U8, "v_s")
        nc.vector.tensor_copy(v_s[:], tab_s[:].bitcast(U8).indirect(offsets[:]))
        v_w0 = sb([P, CHUNK], U32, "v_w0")
        gather_words(0, CHUNK, v_w0[:])
        by_slot = wu_s_raw[:].bitcast(U8).rearrange("p (m t) -> p t m", t=PACK)
        nc.vector.tensor_copy(wu_s[0][:], by_slot[:, 0:2, :])
        nc.vector.tensor_copy(wu_s[1][:], by_slot[:, 2:4, :])
        v_w = placed([P, J - CHUNK], U32, "v_w", 32 * SUM_BYTES + CHUNK)
        gather_words(CHUNK, J, v_w[:])

        picked = {}

        def gather_residual(t, a, z, dst):
            nc.vector.tensor_copy(dst, r_tab[t][:].indirect(listed(a, z)))
            for k in range(a // P, z // P):
                picked[(t, k)] = dst[:, k * P - a : (k + 1) * P - a]

        def later(c):
            rest = slice((c - 1) * CHUNK, c * CHUNK)
            a, z = c * CHUNK, (c + 1) * CHUNK
            return smoothed(c, v_w[:, rest], v_s[:, a:z])

        def step(c, bank_tags, total, plane):
            a, z = c * CHUNK, (c + 1) * CHUNK
            planes = later(c + 1)
            y = [placed([P, CHUNK], F32, "y0_%d" % c, act_at[c + 1][0] * SUM_BYTES)]
            product(0, a, z, y[0][:], bank_tags[0])
            quantise_h(c + 1, weave(c + 1, planes), plane)
            if c == 0:
                window.append(placed([P, T], F32, "window1", 36 * SUM_BYTES))
                nc.gpsimd.memset(window[1][:].bitcast(I32), 0)
            y.append(placed([P, CHUNK], F32, "y1_%d" % c, planes_at[c + 1] * SUM_BYTES))
            product(1, a, z, y[1][:], bank_tags[1])
            for t in range(2):
                add_residual(t, a, z, y[t][:], total[t])
            for t in range(2):
                place(t, a, z, total[t])

        gather_residual(2, 0, J, sb([P, J], F32, "picked2")[:])
        wd_bf = sb([P, WD_HALF, PACK], BF16, "wd_bf0")
        nc.vector.tensor_copy(wd_bf[:], wd_raw[0][:].rearrange("p j n -> p n j"))
        quantise_h(0, weave(0, smoothed(0, v_w0[:], v_s[:, 0:CHUNK])), sb([P, CHUNK], U8, "h_s0"))
        quantise_wd(0, wd_bf[:].rearrange("p n j -> p (n j)"), placed([P, WD_HALF], U32, "wd_w0", 11 * SUM_BYTES)[:])
        gather_residual(3, 0, J, placed([P, J], F32, "picked3", 24 * SUM_BYTES)[:])
        step(
            0,
            [5, 3],
            [sb([P, CHUNK], F32, "total0_0")[:], placed([P, CHUNK], F32, "total1_0", SUM_BYTES // 2)[:]],
            sb([P, CHUNK], U8, "h_s1"),
        )
        step(
            1,
            [5, 1],
            [placed([P, CHUNK], F32, "total0_1", SUM_BYTES)[:], placed([P, CHUNK], F32, "total1_1", 0)[:]],
            sb([P, CHUNK], U8, "h_s2", "total0_0"),
        )

        planes = later(3)
        y = placed([P, CHUNK], F32, "y0_2", act_at[3][0] * SUM_BYTES)
        product(0, HALF, HALF + CHUNK, y[:], 5)
        woven = weave(3, planes)
        total = placed([P, CHUNK], F32, "total0_2", 3 * SUM_BYTES // 2)
        add_residual(0, HALF, HALF + CHUNK, y[:], total[:])
        quantise_h(3, woven, placed([P, CHUNK], U8, "h_s3", 0))
        place(0, HALF, HALF + CHUNK, total[:])
        y = sb([P, CHUNK], F32, "y0_3")
        product(0, J - CHUNK, J, y[:], 5)
        total = placed([P, CHUNK], F32, "total0_3", 22 * SUM_BYTES)
        add_residual(0, J - CHUNK, J, y[:], total[:])
        quantise_wd_tile(2, rounded_wd(2, 3 * SUM_BYTES), sb([P, P], U32, "wd_w2"))
        place(0, J - CHUNK, J, total[:])
        y = sb([P, HALF], F32, "y1_23")
        product(1, HALF, J, y[:], 3)
        total = sb([P, HALF], F32, "total1_23", "y0_3")
        add_residual(1, HALF, J, y[:], total[:])
        quantise_wd_tile(3, rounded_wd(3, 19 * SUM_BYTES), placed([P, P], U32, "wd_w3", 22 * SUM_BYTES))
        place(1, HALF, J, total[:])

        for t in range(2, TILES):
            total = sb([P, J], F32, "late_total%d" % t)
            for i in range(2):
                late_half(t, i, [picked[(t, BLOCKS * i + k)] for k in range(BLOCKS)], total[:, HALF * i : HALF * (i + 1)])
            place(t, 0, J, total[:])
